import numpy as np
import ml_dtypes


def mxq(x, axis, fmt="e4m3"):
    dtype, down = {"e4m3": (ml_dtypes.float8_e4m3fn, 7), "e5m2": (ml_dtypes.float8_e5m2, 14)}[fmt]
    v = np.moveaxis(np.asarray(x, np.float32).astype(ml_dtypes.bfloat16).astype(np.float64), axis, -1)
    blocks = v.reshape(v.shape[:-1] + (-1, 32))
    amax = np.abs(blocks).max(-1, keepdims=True)
    byte = np.maximum(np.where(amax > 0, np.frexp(amax)[1] - 1 + 127, 0) - down, 1)
    scale = np.exp2(byte - 127.0)
    codes = (blocks / scale).astype(np.float32).astype(dtype).astype(np.float64)
    return np.moveaxis((codes * scale).reshape(v.shape), -1, axis)


WIDE = False


def mx_kscale(k):
    if not WIDE:
        return np.ones(k)
    levels = np.array([10, -10, 5, -5, 0])
    if k % 512:
        return np.exp2(np.random.permutation(np.resize(levels, k // 32))).repeat(32)
    a = np.empty((k // 512, 16))
    for p in range(k // 512):
        a[p, :8] = np.random.permutation(np.resize(levels, 8))
        for g in range(8):
            far = levels[np.abs(levels - a[p, g]) >= 10]
            a[p, g + 8] = far[np.random.randint(len(far))]
    return np.exp2(a.ravel()).repeat(32)


def f64(x):
    return np.asarray(x).astype(np.float64)


def striped(idx):
    return np.tile(idx.reshape(-1, 16).T, (8, 1)).astype(np.uint16)


def unstriped(offs):
    return offs[:16].T.reshape(-1).astype(np.int64)


E2M1 = np.array([0.0, 0.5, 1.0, 1.5, 2.0, 3.0, 4.0, 6.0, -0.0, -0.5, -1.0, -1.5, -2.0, -3.0, -4.0, -6.0])


def pack_weight(w, fmt):
    k, n = w.shape
    w = f64(np.asarray(w, np.float32).astype(ml_dtypes.bfloat16)).reshape(k // 32, 32, n)
    amax = np.abs(w).max(1)
    if fmt == "e4m3":
        byte = np.frexp(amax)[1] - 1 + 127 - 7
    else:
        mant, ex = np.frexp(amax / 6.0)
        byte = np.where(mant > 0.5, ex, ex - 1) + 127
    byte = np.clip(np.where(amax > 0, byte, 1), 1, 254)
    scaled = (w * np.exp2(127.0 - byte)[:, None, :]).reshape(k, n).astype(np.float32)
    by_word = np.ascontiguousarray(scaled.reshape(k // 512, 128, 4, n).transpose(0, 1, 3, 2))
    if fmt == "e4m3":
        words = by_word.astype(ml_dtypes.float8_e4m3fn).view(np.uint8)
    else:
        c = by_word.astype(ml_dtypes.float4_e2m1fn).view(np.uint8) & 0xF
        words = (c[..., 0::2] | (c[..., 1::2] << 4)).reshape(k // 512, 128, 2 * n)
    return np.ascontiguousarray(words), np.ascontiguousarray(byte.astype(np.uint8).reshape(k // 512, 16, n))


def unpack_weight(words, scales, fmt):
    g, _, n = scales.shape
    words = np.ascontiguousarray(words).reshape(g, 128, n, -1)
    if fmt == "e4m3":
        vals = words.view(ml_dtypes.float8_e4m3fn).astype(np.float64)
    else:
        nib = np.empty((g, 128, n, 4), np.uint8)
        nib[..., 0::2] = words & 0xF
        nib[..., 1::2] = words >> 4
        vals = E2M1[nib]
    vals = vals * np.repeat(np.exp2(scales.astype(np.float64) - 127.0), 8, axis=1)[..., None]
    return vals.transpose(0, 1, 3, 2).reshape(g * 512, n)


def relu(v):
    return np.maximum(v, 0.0)


K, T, E, C, H, N = 1024, 2048, 8, 128, 512, 256


def by_expert(wq, xq):
    return np.concatenate([wq[e].T @ xq[:, e * C:(e + 1) * C] for e in range(E)], axis=1)


def setup_inputs():
    n = np.random.standard_normal
    s = mx_kscale(K)[:, None]
    u = mx_kscale(H)
    w1 = [pack_weight(m, "e2m1") for m in n((E, K, H)) / np.sqrt(K) / s[None] * u[None, None, :]]
    w2 = [pack_weight(m, "e2m1") for m in n((E, H, N)) / np.sqrt(H) / u[None, :, None]]
    x = pack_weight(n((K, T)) * s, "e4m3")
    return {
        "x_words": x[0],
        "x_scales": x[1],
        "w1_words": np.stack([m[0] for m in w1]),
        "w1_scales": np.stack([m[1] for m in w1]),
        "w2_words": np.stack([m[0] for m in w2]),
        "w2_scales": np.stack([m[1] for m in w2]),
        "gate": np.tile(np.random.uniform(0.2, 1.0, E * C), (N, 1)).astype(np.float32),
        "offs": striped(np.random.permutation(T)[:E * C]),
    }


def reference(x_words, x_scales, w1_words, w1_scales, w2_words, w2_scales, gate, offs):
    idx = unstriped(offs)
    w1 = np.stack([unpack_weight(w1_words[e], w1_scales[e], "e2m1") for e in range(E)])
    w2 = np.stack([unpack_weight(w2_words[e], w2_scales[e], "e2m1") for e in range(E)])
    xq = unpack_weight(x_words, x_scales, "e4m3")[:, idx]
    h = relu(by_expert(w1, xq))
    y = by_expert(w2, mxq(h, 0, "e4m3"))
    out = np.zeros((N, T))
    out[:, idx] = f64(gate) * y
    return out

@@ -1,0 +1,170 @@
+from contextlib import ExitStack
+
+import concourse.mybir as mybir
+from concourse.masks import make_identity
+
+K, T, E, C, H, N = 1024, 2048, 8, 128, 512, 256
+FLOPS = 2 * E * C * (K * H + H * N)
+
+F32 = mybir.dt.float32
+BF16 = mybir.dt.bfloat16
+I32 = mybir.dt.int32
+U32 = mybir.dt.uint32
+U16 = mybir.dt.uint16
+U8 = mybir.dt.uint8
+FP8X4 = mybir.dt.float8_e4m3fn_x4
+FP4X4 = mybir.dt.float4_e2m1fn_x4
+RELU = mybir.ActivationFunctionType.Relu
+MULT = mybir.AluOpType.mult
+
+P = 128
+PASSES = K // 512
+PAIR = 2
+CHUNKS = E // PAIR
+SLOTS = PAIR * C
+HALVES = N // P
+
+
+def load_scale_rows(nc, plane, rows):
+    for r in range(4):
+        nc.sync.dma_start(out=plane[r:P:32], in_=rows[r].bitcast(I32))
+
+
+def tile_moe_pkd_mlp_relu_kernel(tc, x_words, x_scales, w1_words, w1_scales, w2_words, w2_scales, gate, offs, out):
+    nc = tc.nc
+    with ExitStack() as ctx:
+        keep = ctx.enter_context(tc.tile_pool(name="keep", bufs=1))
+        ring = ctx.enter_context(tc.tile_pool(name="ring", bufs=3))
+        psum = ctx.enter_context(tc.psum_pool(name="psum", bufs=1))
+
+        offsets = keep.tile([P, E * C // 16], U16, name="offsets")
+        x_word = [keep.tile([P, T], I32, name="x_word%d" % o, align_bytes=64) for o in range(PASSES)]
+        x_byte = keep.tile([P, PASSES, T // 4], I32, name="x_byte", align_bytes=64)
+        w1_word = [keep.tile([P, PAIR * PASSES, 2 * H], U8, name="w1_word%d" % c, align_bytes=64) for c in range(CHUNKS)]
+        w1_byte = [keep.tile([P, PAIR * PASSES, H // 4], I32, name="w1_byte%d" % c, align_bytes=64) for c in range(CHUNKS)]
+        w2_word = [keep.tile([P, E // 2, 2 * N], U8, name="w2_word%d" % g, align_bytes=64) for g in range(2)]
+        w2_byte = keep.tile([P, E, N // 4], I32, name="w2_byte", align_bytes=64)
+        gate_sb = [keep.tile([P, E * C // 2], F32, name="gate_sb%d" % g) for g in range(2)]
+        window = [keep.tile([P, T], F32, name="window%d" % v) for v in range(HALVES)]
+        gated = [keep.tile([P, E * C], F32, name="gated%d" % v) for v in range(HALVES)]
+        zero = keep.tile([P, 8], F32, name="zero")
+        ident = keep.tile([P, P], F32, name="ident")
+
+        nc.vector.memset(x_byte[:], 0)
+        nc.vector.memset(zero[:], 0.0)
+        for c in range(CHUNKS):
+            nc.vector.memset(w1_byte[c][:], 0)
+        nc.vector.memset(w2_byte[:], 0)
+        make_identity(nc, ident[:])
+        for v in range(HALVES):
+            nc.scalar.activation(out=window[v][:], in_=zero[:, 0:1].to_broadcast([P, T]), func=RELU)
+
+        def load_x(o, parts):
+            src = x_words[o].rearrange("p t r -> p (t r)").bitcast(I32)
+            for a in range(parts):
+                cols = slice(a * T // parts, (a + 1) * T // parts)
+                nc.sync.dma_start(out=x_word[o][:, cols], in_=src[:, cols])
+
+        def load_w1(c):
+            pair = slice(PAIR * c, PAIR * (c + 1))
+            load_scale_rows(nc, w1_byte[c], w1_scales[pair].rearrange("e s (q r) i -> r q (e s) i", r=4))
+            nc.sync.dma_start(out=w1_word[c][:].bitcast(I32), in_=w1_words[pair].rearrange("e s p b -> p (e s) b").bitcast(I32))
+
+        def load_w2(g):
+            four = slice(4 * g, 4 * g + 4)
+            nc.sync.dma_start(out=w2_word[g][:].bitcast(I32), in_=w2_words[four].rearrange("e s p b -> p (e s) b").bitcast(I32))
+            nc.sync.dma_start(out=gate_sb[g][:], in_=gate[0:P, 512 * g : 512 * (g + 1)])
+
+        nc.sync.dma_start(offsets[:], offs)
+        load_x(0, 2)
+        load_scale_rows(nc, x_byte, x_scales.rearrange("o (q r) t -> r q o t", r=4))
+        load_x(1, 1)
+        load_w1(0)
+        load_w1(1)
+        load_scale_rows(nc, w2_byte, w2_scales.rearrange("e s (q r) n -> r q (e s) n", r=4))
+        load_w2(0)
+        load_w1(2)
+        load_w1(3)
+        load_w2(1)
+
+        def chunk_offsets(c):
+            return offsets[:, c * SLOTS // 16 : (c + 1) * SLOTS // 16]
+
+        g_word = {}
+        g_byte = {}
+        h_word = {}
+        h_byte = {}
+
+        def gather(c):
+            for o in range(PASSES):
+                g_word[c, o] = keep.tile([P, SLOTS], U32, name="g_word%d_%d" % (c, o), align_bytes=64)
+                g_byte[c, o] = keep.tile([P, SLOTS], U8, name="g_byte%d_%d" % (c, o), align_bytes=64)
+                nc.vector.tensor_copy(out=g_word[c, o][:], in_=x_word[o][:].bitcast(U32).indirect(chunk_offsets(c)))
+                nc.vector.tensor_copy(out=g_byte[c, o][:], in_=x_byte[:, o, :].bitcast(U8).indirect(chunk_offsets(c)))
+
+        def first_layer(c):
+            h_bf = ring.tile([P, SLOTS, 4], BF16, name="h_bf", align_bytes=64)
+            relu = []
+            for m in range(PAIR):
+                cols = slice(m * C, (m + 1) * C)
+                acc = psum.tile([P, H], F32, name="acc", bufs=3)
+                for o in range(PASSES):
+                    nc.tensor.matmul_mx(
+                        out=acc[:],
+                        lhsT=g_word[c, o][:, cols].bitcast(FP8X4),
+                        lhsT_scale=g_byte[c, o][:, cols],
+                        rhs=w1_word[c][:, PASSES * m + o, :].bitcast(FP4X4),
+                        rhs_scale=w1_byte[c][:, PASSES * m + o, :].bitcast(U8),
+                        start=(o == 0),
+                        stop=(o == PASSES - 1),
+                    )
+                by_slot = ring.tile([P, 2, P, 2], BF16, name="by_slot", bufs=4, align_bytes=64)
+                nc.scalar.activation(out=by_slot[:], in_=acc[:].rearrange("j (p u d) -> j u p d", u=2, d=2), func=RELU)
+                relu.append(by_slot)
+            for m in range(PAIR):
+                turned = psum.tile([P, 2, C], F32, name="turned", bufs=2)
+                pairs = relu[m][:].rearrange("j u p d -> j (u p d)").bitcast(F32)
+                for u in range(2):
+                    nc.tensor.transpose(turned[:, u, :], pairs[:, u * P : (u + 1) * P], ident[:])
+                nc.scalar.copy(out=h_bf[:, m * C : (m + 1) * C, :].bitcast(F32), in_=turned[:].rearrange("p u j -> p j u"))
+            h_word[c] = ring.tile([P, SLOTS], U32, name="h_word", align_bytes=64)
+            h_byte[c] = ring.tile([P, SLOTS], U8, name="h_byte", align_bytes=64)
+            nc.vector.quantize_mx(out=h_word[c][:].bitcast(FP8X4), scales=h_byte[c][:], in_=h_bf[:].rearrange("p j t -> p (j t)"))
+
+        def second_layer(c):
+            y = psum.tile([P, HALVES, SLOTS], F32, name="y", bufs=2)
+            for v in range(HALVES):
+                for m in range(PAIR):
+                    e = PAIR * c + m
+                    cols = slice(m * C, (m + 1) * C)
+                    nc.tensor.matmul_mx(
+                        out=y[:, v, cols],
+                        lhsT=w2_word[e // 4][:, e % 4, 2 * P * v : 2 * P * (v + 1)].bitcast(FP4X4),
+                        lhsT_scale=w2_byte[:, e, :].bitcast(U8)[:, P * v : P * (v + 1)],
+                        rhs=h_word[c][:, cols].bitcast(FP8X4),
+                        rhs_scale=h_byte[c][:, cols],
+                        start=True,
+                        stop=True,
+                    )
+            g0 = (c % 2) * SLOTS
+            for v in range(HALVES):
+                nc.vector.tensor_tensor(
+                    out=gated[v][:, c * SLOTS : (c + 1) * SLOTS], in0=y[:, v, :], in1=gate_sb[c // 2][:, g0 : g0 + SLOTS], op=MULT
+                )
+
+        def scatter(c, v):
+            nc.vector.tensor_copy(out=window[v][:].indirect(chunk_offsets(c)), in_=gated[v][:, c * SLOTS : (c + 1) * SLOTS])
+
+        for step in range(CHUNKS + 2):
+            if step >= 2:
+                second_layer(step - 2)
+            if 1 <= step <= CHUNKS:
+                first_layer(step - 1)
+            if step < CHUNKS:
+                gather(step)
+            if step >= 2:
+                scatter(step - 2, 0)
+        nc.sync.dma_start(out=out[0:P, :], in_=window[0][:])
+        for c in range(CHUNKS):
+            scatter(c, 1)
+        nc.sync.dma_start(out=out[P : 2 * P, :], in_=window[1][:])

@@ -15,156 +15,197 @@ U8 = mybir.dt.uint8
 FP8X4 = mybir.dt.float8_e4m3fn_x4
 FP4X4 = mybir.dt.float4_e2m1fn_x4
 RELU = mybir.ActivationFunctionType.Relu
+COPY = mybir.ActivationFunctionType.Copy
 MULT = mybir.AluOpType.mult
 
 P = 128
 PASSES = K // 512
-PAIR = 2
-CHUNKS = E // PAIR
-SLOTS = PAIR * C
-HALVES = N // P
+CLEAR = 512
+MOVED = 112
+WORD_RUNS = [[(0, 2), (2, 5), (5, 8)], [(0, 2), (2, 4), (4, 6), (6, 8)]]
+W1_WORD_RUNS = [(1, 2), (0, 1), (2, 3), (3, 4), (4, 6), (6, 8)]
+W1_BYTE_RUNS = [(0, 2), (2, 4), (4, 8)]
+W2_WORD_RUNS = [(0, 2), (2, 8)]
+W2_BYTE_RUNS = [(0, 2), (2, 8)]
+LOADS = [("s", 0, 2), ("X",), ("w", 1, 2), ("w", 0, 1), ("s", 2, 4), ("h",), ("w", 2, 3), ("G", 0, 4), ("w", 3, 4), ("x", 0, 2), ("w", 4, 6), ("s", 4, 8), ("x", 2, 8), ("v", 2, 8), ("w", 6, 8), ("G", 4, 8)]
+STAGES = [("f", 0), ("f", 1), ("t", 0), ("t", 1), ("q", 0), ("n", 0, 0, "y"), ("f", 2), ("f", 3), ("t", 2), ("t", 3), ("q", 1), ("n", 0, 1, "acc0"), ("n", 1, 0, "y"), ("f", 4), ("f", 5), ("t", 4), ("t", 5), ("q", 2), ("n", 1, 1, "turn1"), ("n", 2, 0, "turn1"), ("f", 6), ("f", 7), ("t", 6), ("t", 7), ("q", 3), ("n", 2, 1, "acc1"), ("n", 3, 0, "y"), ("n", 3, 1, "y")]
+CODE_SLOTS = ["", "", "", ""]
+RELU_ON_VECTOR = ()
+TURN_ON_VECTOR = (1, 2, 3)
+Y_ON_VECTOR = ()
 
 
-def load_scale_rows(nc, plane, rows):
-    for r in range(4):
-        nc.sync.dma_start(out=plane[r:P:32], in_=rows[r].bitcast(I32))
+def run_of(runs, e):
+    return [run for run in runs if run[0] <= e < run[1]][0]
 
 
 def tile_moe_pkd_mlp_relu_kernel(tc, x_words, x_scales, w1_words, w1_scales, w2_words, w2_scales, gate, offs, out):
     nc = tc.nc
     with ExitStack() as ctx:
         keep = ctx.enter_context(tc.tile_pool(name="keep", bufs=1))
-        ring = ctx.enter_context(tc.tile_pool(name="ring", bufs=3))
         psum = ctx.enter_context(tc.psum_pool(name="psum", bufs=1))
 
+        def held(shape, dtype, name, tag=""):
+            return keep.tile(shape, dtype, name=name, tag=tag or name, align_bytes=64)
+
+        def bank(shape, name, tag):
+            return psum.tile(shape, F32, name=name, tag=tag, bufs=3 if tag == "y" else 1)
+
         offsets = keep.tile([P, E * C // 16], U16, name="offsets")
-        x_word = [keep.tile([P, T], I32, name="x_word%d" % o, align_bytes=64) for o in range(PASSES)]
-        x_byte = keep.tile([P, PASSES, T // 4], I32, name="x_byte", align_bytes=64)
-        w1_word = [keep.tile([P, PAIR * PASSES, 2 * H], U8, name="w1_word%d" % c, align_bytes=64) for c in range(CHUNKS)]
-        w1_byte = [keep.tile([P, PAIR * PASSES, H // 4], I32, name="w1_byte%d" % c, align_bytes=64) for c in range(CHUNKS)]
-        w2_word = [keep.tile([P, E // 2, 2 * N], U8, name="w2_word%d" % g, align_bytes=64) for g in range(2)]
-        w2_byte = keep.tile([P, E, N // 4], I32, name="w2_byte", align_bytes=64)
-        gate_sb = [keep.tile([P, E * C // 2], F32, name="gate_sb%d" % g) for g in range(2)]
-        window = [keep.tile([P, T], F32, name="window%d" % v) for v in range(HALVES)]
-        gated = [keep.tile([P, E * C], F32, name="gated%d" % v) for v in range(HALVES)]
-        zero = keep.tile([P, 8], F32, name="zero")
-        ident = keep.tile([P, P], F32, name="ident")
+        x_word = [held([P, T], I32, "x_word%d" % o) for o in range(PASSES)]
+        x_byte = held([P, T // 4], I32, "x_byte")
+        w1_word = {run: held([P, PASSES * (run[1] - run[0]), H // 2], I32, "w1_word%d" % run[0]) for run in W1_WORD_RUNS}
+        w1_byte = {run: held([P, PASSES * (run[1] - run[0]), H // 4], I32, "w1_byte%d" % run[0]) for run in W1_BYTE_RUNS}
+        w2_word = {run: held([P, run[1] - run[0], N // 2], I32, "w2_word%d" % run[0]) for run in W2_WORD_RUNS}
+        w2_byte = {run: held([P, run[1] - run[0], N // 4], I32, "w2_byte%d" % run[0]) for run in W2_BYTE_RUNS}
+        g_byte = [held([P, E * C], U8, "g_byte0"), held([P, E * C // 4], I32, "g_byte1")]
+        gate_sb = [held([P, 4 * C], F32, "gate_sb%d" % g) for g in range(2)]
+        window = [held([P, T], F32, "window%d" % v) for v in range(2)]
+        zero = held([P, 8], F32, "zero")
+        ident = held([P, P], F32, "ident")
 
-        nc.vector.memset(x_byte[:], 0)
-        nc.vector.memset(zero[:], 0.0)
-        for c in range(CHUNKS):
-            nc.vector.memset(w1_byte[c][:], 0)
-        nc.vector.memset(w2_byte[:], 0)
+        nc.gpsimd.memset(x_byte[:], 0)
         make_identity(nc, ident[:])
-        for v in range(HALVES):
-            nc.scalar.activation(out=window[v][:], in_=zero[:, 0:1].to_broadcast([P, T]), func=RELU)
+        nc.vector.memset(zero[:], 0.0)
+        nc.vector.memset(g_byte[1][:], 0)
+        for run in W1_BYTE_RUNS:
+            nc.vector.memset(w1_byte[run][:], 0)
+        for run in W2_BYTE_RUNS:
+            nc.vector.memset(w2_byte[run][:], 0)
 
-        def load_x(o, parts):
-            src = x_words[o].rearrange("p t r -> p (t r)").bitcast(I32)
-            for a in range(parts):
-                cols = slice(a * T // parts, (a + 1) * T // parts)
-                nc.sync.dma_start(out=x_word[o][:, cols], in_=src[:, cols])
+        def load_words(tile, words, run):
+            nc.sync.dma_start(out=tile[:], in_=words[run[0] : run[1]].rearrange("e s p b -> p (e s) b").bitcast(I32))
 
-        def load_w1(c):
-            pair = slice(PAIR * c, PAIR * (c + 1))
-            load_scale_rows(nc, w1_byte[c], w1_scales[pair].rearrange("e s (q r) i -> r q (e s) i", r=4))
-            nc.sync.dma_start(out=w1_word[c][:].bitcast(I32), in_=w1_words[pair].rearrange("e s p b -> p (e s) b").bitcast(I32))
+        def load_scales(plane, scales, run):
+            rows = scales[run[0] : run[1]].rearrange("e s (q r) i -> r q (e s) i", r=4)
+            for r in range(4):
+                nc.sync.dma_start(out=plane[r:P:32], in_=rows[r].bitcast(I32))
 
-        def load_w2(g):
-            four = slice(4 * g, 4 * g + 4)
-            nc.sync.dma_start(out=w2_word[g][:].bitcast(I32), in_=w2_words[four].rearrange("e s p b -> p (e s) b").bitcast(I32))
-            nc.sync.dma_start(out=gate_sb[g][:], in_=gate[0:P, 512 * g : 512 * (g + 1)])
+        def load_tokens(o):
+            nc.sync.dma_start(out=x_word[o][:], in_=x_words[o].rearrange("p t r -> p (t r)").bitcast(I32))
+
+        def gather_bytes():
+            nc.vector.tensor_copy(out=g_byte[0][:], in_=x_byte[:].bitcast(U8).indirect(offsets[:]))
+
+        def shift(engine):
+            engine.dma_start(out=g_byte[1][0:MOVED, :], in_=g_byte[0][4 : 4 + MOVED, :].bitcast(I32))
 
         nc.sync.dma_start(offsets[:], offs)
-        load_x(0, 2)
-        load_scale_rows(nc, x_byte, x_scales.rearrange("o (q r) t -> r q o t", r=4))
-        load_x(1, 1)
-        load_w1(0)
-        load_w1(1)
-        load_scale_rows(nc, w2_byte, w2_scales.rearrange("e s (q r) n -> r q (e s) n", r=4))
-        load_w2(0)
-        load_w1(2)
-        load_w1(3)
-        load_w2(1)
+        load_words(w2_word[0, 2], w2_words, (0, 2))
+        for q in range(4):
+            nc.sync.dma_start(out=x_byte[32 * q : 32 * q + 8, :], in_=x_scales[:, 4 * q : 4 * q + 4, :].bitcast(I32))
+        load_tokens(0)
+        gather_bytes()
+        for step in LOADS:
+            run = step[1:]
+            if step[0] == "X":
+                load_tokens(1)
+            elif step[0] == "h":
+                shift(nc.sync)
+            elif step[0] == "s":
+                load_scales(w1_byte[run], w1_scales, run)
+            elif step[0] == "w":
+                load_words(w1_word[run], w1_words, run)
+            elif step[0] == "x":
+                load_scales(w2_byte[run], w2_scales, run)
+            elif step[0] == "v":
+                load_words(w2_word[run], w2_words, run)
+            else:
+                nc.sync.dma_start(out=gate_sb[run[0] // 4][:], in_=gate[0:P, C * run[0] : C * run[1]])
+        token_scale = [g_byte[0][:], g_byte[1][:].bitcast(U8)]
+        late_zero = zero
 
-        def chunk_offsets(c):
-            return offsets[:, c * SLOTS // 16 : (c + 1) * SLOTS // 16]
+        def slots_of(run):
+            return offsets[:, run[0] * C // 16 : run[1] * C // 16]
 
         g_word = {}
-        g_byte = {}
+        for o in range(PASSES):
+            for run in WORD_RUNS[o]:
+                g_word[o, run] = held([P, (run[1] - run[0]) * C], U32, "g_word%d_%d" % (o, run[0]))
+                nc.vector.tensor_copy(out=g_word[o, run][:], in_=x_word[o][:].bitcast(U32).indirect(slots_of(run)))
+
+        for v in (0, 1):
+            for a in range(0, T, CLEAR):
+                src = late_zero if v == 1 else zero
+                nc.scalar.activation(out=window[v][:, a : a + CLEAR], in_=src[:, 0:1].to_broadcast([P, CLEAR]), func=RELU)
+
+        by_slot = {}
+        h_bf = [held([P, 2, C, 4], BF16, "h_bf%d" % c) for c in range(E // 2)]
         h_word = {}
         h_byte = {}
 
-        def gather(c):
+        def first_layer(e):
+            acc = bank([P, H], "acc", "acc%d" % (e % 3))
+            words, bytes_run = run_of(W1_WORD_RUNS, e), run_of(W1_BYTE_RUNS, e)
             for o in range(PASSES):
-                g_word[c, o] = keep.tile([P, SLOTS], U32, name="g_word%d_%d" % (c, o), align_bytes=64)
-                g_byte[c, o] = keep.tile([P, SLOTS], U8, name="g_byte%d_%d" % (c, o), align_bytes=64)
-                nc.vector.tensor_copy(out=g_word[c, o][:], in_=x_word[o][:].bitcast(U32).indirect(chunk_offsets(c)))
-                nc.vector.tensor_copy(out=g_byte[c, o][:], in_=x_byte[:, o, :].bitcast(U8).indirect(chunk_offsets(c)))
-
-        def first_layer(c):
-            h_bf = ring.tile([P, SLOTS, 4], BF16, name="h_bf", align_bytes=64)
-            relu = []
-            for m in range(PAIR):
-                cols = slice(m * C, (m + 1) * C)
-                acc = psum.tile([P, H], F32, name="acc", bufs=3)
-                for o in range(PASSES):
-                    nc.tensor.matmul_mx(
-                        out=acc[:],
-                        lhsT=g_word[c, o][:, cols].bitcast(FP8X4),
-                        lhsT_scale=g_byte[c, o][:, cols],
-                        rhs=w1_word[c][:, PASSES * m + o, :].bitcast(FP4X4),
-                        rhs_scale=w1_byte[c][:, PASSES * m + o, :].bitcast(U8),
-                        start=(o == 0),
-                        stop=(o == PASSES - 1),
-                    )
-                by_slot = ring.tile([P, 2, P, 2], BF16, name="by_slot", bufs=4, align_bytes=64)
-                nc.scalar.activation(out=by_slot[:], in_=acc[:].rearrange("j (p u d) -> j u p d", u=2, d=2), func=RELU)
-                relu.append(by_slot)
-            for m in range(PAIR):
-                turned = psum.tile([P, 2, C], F32, name="turned", bufs=2)
-                pairs = relu[m][:].rearrange("j u p d -> j (u p d)").bitcast(F32)
-                for u in range(2):
-                    nc.tensor.transpose(turned[:, u, :], pairs[:, u * P : (u + 1) * P], ident[:])
-                nc.scalar.copy(out=h_bf[:, m * C : (m + 1) * C, :].bitcast(F32), in_=turned[:].rearrange("p u j -> p j u"))
-            h_word[c] = ring.tile([P, SLOTS], U32, name="h_word", align_bytes=64)
-            h_byte[c] = ring.tile([P, SLOTS], U8, name="h_byte", align_bytes=64)
-            nc.vector.quantize_mx(out=h_word[c][:].bitcast(FP8X4), scales=h_byte[c][:], in_=h_bf[:].rearrange("p j t -> p (j t)"))
-
-        def second_layer(c):
-            y = psum.tile([P, HALVES, SLOTS], F32, name="y", bufs=2)
-            for v in range(HALVES):
-                for m in range(PAIR):
-                    e = PAIR * c + m
-                    cols = slice(m * C, (m + 1) * C)
-                    nc.tensor.matmul_mx(
-                        out=y[:, v, cols],
-                        lhsT=w2_word[e // 4][:, e % 4, 2 * P * v : 2 * P * (v + 1)].bitcast(FP4X4),
-                        lhsT_scale=w2_byte[:, e, :].bitcast(U8)[:, P * v : P * (v + 1)],
-                        rhs=h_word[c][:, cols].bitcast(FP8X4),
-                        rhs_scale=h_byte[c][:, cols],
-                        start=True,
-                        stop=True,
-                    )
-            g0 = (c % 2) * SLOTS
-            for v in range(HALVES):
-                nc.vector.tensor_tensor(
-                    out=gated[v][:, c * SLOTS : (c + 1) * SLOTS], in0=y[:, v, :], in1=gate_sb[c // 2][:, g0 : g0 + SLOTS], op=MULT
+                run = run_of(WORD_RUNS[o], e)
+                nc.tensor.matmul_mx(
+                    out=acc[:],
+                    lhsT=g_word[o, run][:, (e - run[0]) * C : (e - run[0] + 1) * C].bitcast(FP8X4),
+                    lhsT_scale=token_scale[o][:, e * C : (e + 1) * C],
+                    rhs=w1_word[words][:, PASSES * (e - words[0]) + o, :].bitcast(FP4X4),
+                    rhs_scale=w1_byte[bytes_run][:, PASSES * (e - bytes_run[0]) + o, :].bitcast(U8),
+                    start=(o == 0),
+                    stop=(o == PASSES - 1),
                 )
+            by_slot[e] = held([P, 2, P, 2], BF16, "by_slot%d" % e)
+            sums = acc[:].rearrange("j (p u d) -> j u p d", u=2, d=2)
+            if e in RELU_ON_VECTOR:
+                nc.vector.tensor_scalar_max(by_slot[e][:], sums, 0.0)
+            else:
+                nc.scalar.activation(out=by_slot[e][:], in_=sums, func=RELU)
 
-        def scatter(c, v):
-            nc.vector.tensor_copy(out=window[v][:].indirect(chunk_offsets(c)), in_=gated[v][:, c * SLOTS : (c + 1) * SLOTS])
+        def turn(e):
+            turned = bank([P, 2, C], "turned", "turn%d" % (e % 2))
+            pairs = by_slot[e][:].rearrange("j u p d -> j (u p d)").bitcast(F32)
+            for u in range(2):
+                nc.tensor.transpose(turned[:, u, :], pairs[:, u * P : (u + 1) * P], ident[:])
+            dst, src = h_bf[e // 2][:, e % 2].bitcast(F32), turned[:].rearrange("p u j -> p j u")
+            if e in TURN_ON_VECTOR:
+                nc.vector.tensor_copy(out=dst, in_=src)
+            else:
+                nc.scalar.copy(out=dst, in_=src)
 
-        for step in range(CHUNKS + 2):
-            if step >= 2:
-                second_layer(step - 2)
-            if 1 <= step <= CHUNKS:
-                first_layer(step - 1)
-            if step < CHUNKS:
-                gather(step)
-            if step >= 2:
-                scatter(step - 2, 0)
-        nc.sync.dma_start(out=out[0:P, :], in_=window[0][:])
-        for c in range(CHUNKS):
-            scatter(c, 1)
-        nc.sync.dma_start(out=out[P : 2 * P, :], in_=window[1][:])
+        def quantise(c):
+            parts = [(0, 1), (1, 2)] if c == 0 and False else [(0, 2)]
+            for a, b in parts:
+                words = held([P, (b - a) * C], U32, "h_word%d_%d" % (c, a), CODE_SLOTS[c] if b == 2 else "")
+                scales = held([P, (b - a) * C], U8, "h_byte%d_%d" % (c, a))
+                nc.vector.quantize_mx(out=words[:].bitcast(FP8X4), scales=scales[:], in_=h_bf[c][:, a:b].rearrange("p m j t -> p (m j t)"))
+                for m in range(a, b):
+                    h_word[2 * c + m] = words[:, (m - a) * C : (m - a + 1) * C]
+                    h_byte[2 * c + m] = scales[:, (m - a) * C : (m - a + 1) * C]
+
+        def second_layer(c, v, tag):
+            y = bank([P, 2, C], "y", tag)
+            for m in range(2):
+                e = 2 * c + m
+                words, bytes_run = run_of(W2_WORD_RUNS, e), run_of(W2_BYTE_RUNS, e)
+                nc.tensor.matmul_mx(
+                    out=y[:, m, :],
+                    lhsT=w2_word[words][:, e - words[0], v * P // 2 : (v + 1) * P // 2].bitcast(FP4X4),
+                    lhsT_scale=w2_byte[bytes_run][:, e - bytes_run[0], v * P // 4 : (v + 1) * P // 4].bitcast(U8),
+                    rhs=h_word[e].bitcast(FP8X4),
+                    rhs_scale=h_byte[e],
+                    start=True,
+                    stop=True,
+                )
+            y_sb = held([P, 2 * C], F32, "y_sb%d_%d" % (c, v))
+            if (c, v) in Y_ON_VECTOR:
+                nc.vector.tensor_copy(out=y_sb[:], in_=y[:].rearrange("p m j -> p (m j)"))
+            else:
+                nc.scalar.copy(out=y_sb[:], in_=y[:].rearrange("p m j -> p (m j)"))
+            gate_cols = gate_sb[c // 2][:, 2 * C * (c % 2) : 2 * C * (c % 2 + 1)]
+            nc.vector.tensor_tensor(out=window[v][:].indirect(slots_of((2 * c, 2 * c + 2))), in0=y_sb[:], in1=gate_cols, op=MULT)
+            if c == E // 2 - 1:
+                nc.sync.dma_start(out=out[v * P : (v + 1) * P, :], in_=window[v][:])
+
+        for step in STAGES:
+            if step[0] == "f":
+                first_layer(step[1])
+            elif step[0] == "t":
+                turn(step[1])
+            elif step[0] == "q":
+                quantise(step[1])
+            else:
+                second_layer(step[1], step[2], step[3])

@@ -15,24 +15,19 @@ U8 = mybir.dt.uint8
 FP8X4 = mybir.dt.float8_e4m3fn_x4
 FP4X4 = mybir.dt.float4_e2m1fn_x4
 RELU = mybir.ActivationFunctionType.Relu
-COPY = mybir.ActivationFunctionType.Copy
 MULT = mybir.AluOpType.mult
 
 P = 128
 PASSES = K // 512
+BANK = 512
 CLEAR = 512
-MOVED = 112
-WORD_RUNS = [[(0, 2), (2, 5), (5, 8)], [(0, 2), (2, 4), (4, 6), (6, 8)]]
-W1_WORD_RUNS = [(1, 2), (0, 1), (2, 3), (3, 4), (4, 6), (6, 8)]
+SHIFT = 16
+WORD_RUNS = [[(0, 4), (4, 8)], [(0, 2), (2, 4), (4, 8)]]
+W1_WORD_RUNS = [(0, 1), (1, 2), (2, 3), (3, 4), (4, 6), (6, 8)]
 W1_BYTE_RUNS = [(0, 2), (2, 4), (4, 8)]
-W2_WORD_RUNS = [(0, 2), (2, 8)]
-W2_BYTE_RUNS = [(0, 2), (2, 8)]
-LOADS = [("s", 0, 2), ("X",), ("w", 1, 2), ("w", 0, 1), ("s", 2, 4), ("h",), ("w", 2, 3), ("G", 0, 4), ("w", 3, 4), ("x", 0, 2), ("w", 4, 6), ("s", 4, 8), ("x", 2, 8), ("v", 2, 8), ("w", 6, 8), ("G", 4, 8)]
-STAGES = [("f", 0), ("f", 1), ("t", 0), ("t", 1), ("q", 0), ("n", 0, 0, "y"), ("f", 2), ("f", 3), ("t", 2), ("t", 3), ("q", 1), ("n", 0, 1, "acc0"), ("n", 1, 0, "y"), ("f", 4), ("f", 5), ("t", 4), ("t", 5), ("q", 2), ("n", 1, 1, "turn1"), ("n", 2, 0, "turn1"), ("f", 6), ("f", 7), ("t", 6), ("t", 7), ("q", 3), ("n", 2, 1, "acc1"), ("n", 3, 0, "y"), ("n", 3, 1, "y")]
-CODE_SLOTS = ["", "", "", ""]
-RELU_ON_VECTOR = ()
-TURN_ON_VECTOR = (1, 2, 3)
-Y_ON_VECTOR = ()
+W2_WORD_RUNS = [(0, 2), (2, 4), (4, 8)]
+GATE_RUNS = [(0, 2), (2, 4), (4, 8)]
+SCATTERS = [((0, 2), 0), ((0, 2), 1), ((2, 4), 0), ((2, 4), 1), ((4, 6), 0), ((6, 8), 0), ((4, 8), 1)]
 
 
 def run_of(runs, e):
@@ -45,33 +40,34 @@ def tile_moe_pkd_mlp_relu_kernel(tc, x_words, x_scales, w1_words, w1_scales, w2_
         keep = ctx.enter_context(tc.tile_pool(name="keep", bufs=1))
         psum = ctx.enter_context(tc.psum_pool(name="psum", bufs=1))
 
-        def held(shape, dtype, name, tag=""):
-            return keep.tile(shape, dtype, name=name, tag=tag or name, align_bytes=64)
-
-        def bank(shape, name, tag):
-            return psum.tile(shape, F32, name=name, tag=tag, bufs=3 if tag == "y" else 1)
+        def held(shape, dtype, name):
+            return keep.tile(shape, dtype, name=name, align_bytes=64)
 
         offsets = keep.tile([P, E * C // 16], U16, name="offsets")
-        x_word = [held([P, T], I32, "x_word%d" % o) for o in range(PASSES)]
+        x_word = held([P, PASSES * T], I32, "x_word")
         x_byte = held([P, T // 4], I32, "x_byte")
         w1_word = {run: held([P, PASSES * (run[1] - run[0]), H // 2], I32, "w1_word%d" % run[0]) for run in W1_WORD_RUNS}
         w1_byte = {run: held([P, PASSES * (run[1] - run[0]), H // 4], I32, "w1_byte%d" % run[0]) for run in W1_BYTE_RUNS}
         w2_word = {run: held([P, run[1] - run[0], N // 2], I32, "w2_word%d" % run[0]) for run in W2_WORD_RUNS}
-        w2_byte = {run: held([P, run[1] - run[0], N // 4], I32, "w2_byte%d" % run[0]) for run in W2_BYTE_RUNS}
+        w2_byte = held([P, E, N // 4], I32, "w2_byte")
         g_byte = [held([P, E * C], U8, "g_byte0"), held([P, E * C // 4], I32, "g_byte1")]
-        gate_sb = [held([P, 4 * C], F32, "gate_sb%d" % g) for g in range(2)]
+        gate_sb = {run: held([P, (run[1] - run[0]) * C], F32, "gate_sb%d" % run[0]) for run in GATE_RUNS}
         window = [held([P, T], F32, "window%d" % v) for v in range(2)]
         zero = held([P, 8], F32, "zero")
         ident = held([P, P], F32, "ident")
+        acc_bank = [psum.tile([P, BANK], F32, name="acc_bank%d" % b) for b in range(4)]
+        y_bank = [psum.tile([P, BANK], F32, name="y_bank%d" % b) for b in range(2)]
+        turn_bank = [psum.tile([P, BANK], F32, name="turn_bank%d" % b) for b in range(2)]
 
-        nc.gpsimd.memset(x_byte[:], 0)
-        make_identity(nc, ident[:])
+        nc.gpsimd.memset(x_byte[:, 0 : T // 8], 0)
+        nc.vector.memset(x_byte[:, T // 8 : T // 4], 0)
         nc.vector.memset(zero[:], 0.0)
+        nc.vector.memset(w1_byte[0, 2][:], 0)
         nc.vector.memset(g_byte[1][:], 0)
-        for run in W1_BYTE_RUNS:
-            nc.vector.memset(w1_byte[run][:], 0)
-        for run in W2_BYTE_RUNS:
-            nc.vector.memset(w2_byte[run][:], 0)
+        nc.vector.memset(w1_byte[2, 4][:], 0)
+        nc.vector.memset(w2_byte[:], 0)
+        make_identity(nc, ident[:])
+        nc.gpsimd.memset(w1_byte[4, 8][:], 0)
 
         def load_words(tile, words, run):
             nc.sync.dma_start(out=tile[:], in_=words[run[0] : run[1]].rearrange("e s p b -> p (e s) b").bitcast(I32))
@@ -82,60 +78,62 @@ def tile_moe_pkd_mlp_relu_kernel(tc, x_words, x_scales, w1_words, w1_scales, w2_
                 nc.sync.dma_start(out=plane[r:P:32], in_=rows[r].bitcast(I32))
 
         def load_tokens(o):
-            nc.sync.dma_start(out=x_word[o][:], in_=x_words[o].rearrange("p t r -> p (t r)").bitcast(I32))
+            nc.sync.dma_start(out=x_word[:, o * T : (o + 1) * T], in_=x_words[o].rearrange("p t r -> p (t r)").bitcast(I32))
 
-        def gather_bytes():
-            nc.vector.tensor_copy(out=g_byte[0][:], in_=x_byte[:].bitcast(U8).indirect(offsets[:]))
-
-        def shift(engine):
-            engine.dma_start(out=g_byte[1][0:MOVED, :], in_=g_byte[0][4 : 4 + MOVED, :].bitcast(I32))
-
-        nc.sync.dma_start(offsets[:], offs)
-        load_words(w2_word[0, 2], w2_words, (0, 2))
-        for q in range(4):
-            nc.sync.dma_start(out=x_byte[32 * q : 32 * q + 8, :], in_=x_scales[:, 4 * q : 4 * q + 4, :].bitcast(I32))
-        load_tokens(0)
-        gather_bytes()
-        for step in LOADS:
-            run = step[1:]
-            if step[0] == "X":
-                load_tokens(1)
-            elif step[0] == "h":
-                shift(nc.sync)
-            elif step[0] == "s":
-                load_scales(w1_byte[run], w1_scales, run)
-            elif step[0] == "w":
-                load_words(w1_word[run], w1_words, run)
-            elif step[0] == "x":
-                load_scales(w2_byte[run], w2_scales, run)
-            elif step[0] == "v":
-                load_words(w2_word[run], w2_words, run)
-            else:
-                nc.sync.dma_start(out=gate_sb[run[0] // 4][:], in_=gate[0:P, C * run[0] : C * run[1]])
-        token_scale = [g_byte[0][:], g_byte[1][:].bitcast(U8)]
-        late_zero = zero
+        def load_gate(run):
+            nc.sync.dma_start(out=gate_sb[run][:], in_=gate[0:P, C * run[0] : C * run[1]])
 
         def slots_of(run):
             return offsets[:, run[0] * C // 16 : run[1] * C // 16]
 
+        nc.sync.dma_start(offsets[:], offs)
+        token_rows = x_scales.rearrange("o (q r) t -> r q o t", r=4)
+        for r in range(4):
+            nc.sync.dma_start(out=x_byte[r:P:SHIFT, :], in_=token_rows[r].bitcast(I32))
+        load_tokens(0)
+        nc.vector.tensor_copy(out=g_byte[0][:], in_=x_byte[:].bitcast(U8).indirect(offsets[:]))
+        load_scales(w1_byte[0, 2], w1_scales, (0, 2))
+        load_tokens(1)
+        load_words(w1_word[0, 1], w1_words, (0, 1))
+        nc.sync.dma_start(out=g_byte[1][0 : P - SHIFT, :], in_=g_byte[0][SHIFT:P, :].bitcast(I32))
+        load_words(w1_word[1, 2], w1_words, (1, 2))
+        load_scales(w1_byte[2, 4], w1_scales, (2, 4))
+        load_words(w1_word[2, 3], w1_words, (2, 3))
+        load_scales(w2_byte, w2_scales, (0, E))
+        load_words(w2_word[0, 2], w2_words, (0, 2))
+        load_words(w1_word[3, 4], w1_words, (3, 4))
+        load_gate((0, 2))
+        load_scales(w1_byte[4, 8], w1_scales, (4, 8))
+        load_words(w1_word[4, 6], w1_words, (4, 6))
+        load_words(w2_word[2, 4], w2_words, (2, 4))
+        load_gate((2, 4))
+        load_words(w1_word[6, 8], w1_words, (6, 8))
+        load_words(w2_word[4, 8], w2_words, (4, 8))
+        load_gate((4, 8))
+        token_scale = [g_byte[0][:], g_byte[1][:].bitcast(U8)]
+
         g_word = {}
-        for o in range(PASSES):
-            for run in WORD_RUNS[o]:
-                g_word[o, run] = held([P, (run[1] - run[0]) * C], U32, "g_word%d_%d" % (o, run[0]))
-                nc.vector.tensor_copy(out=g_word[o, run][:], in_=x_word[o][:].bitcast(U32).indirect(slots_of(run)))
 
-        for v in (0, 1):
+        def gather_words(o, run, columns, tag):
+            g_word[o, run] = keep.tile([P, (run[1] - run[0]) * C], U32, name="g_word%d_%d" % (o, run[0]), tag=tag, align_bytes=64)
+            nc.vector.tensor_copy(out=g_word[o, run][:], in_=x_word[:, o * T : o * T + columns].bitcast(U32).indirect(slots_of(run)))
+
+        gather_words(0, (0, 4), T, "g_a")
+        gather_words(1, (0, 2), T, "g_b")
+        gather_words(1, (2, 4), T, "g_c")
+        gather_words(0, (4, 8), PASSES * T, "g_d")
+
+        for v in range(2):
             for a in range(0, T, CLEAR):
-                src = late_zero if v == 1 else zero
-                nc.scalar.activation(out=window[v][:, a : a + CLEAR], in_=src[:, 0:1].to_broadcast([P, CLEAR]), func=RELU)
+                nc.scalar.activation(out=window[v][:, a : a + CLEAR], in_=zero[:, 0:1].to_broadcast([P, CLEAR]), func=RELU)
 
-        by_slot = {}
-        h_bf = [held([P, 2, C, 4], BF16, "h_bf%d" % c) for c in range(E // 2)]
-        h_word = {}
-        h_byte = {}
+        by_slot = [held([P, 2, P, 2], BF16, "by_slot%d" % e) for e in range(E)]
+        h_bf = [keep.tile([P, 2, C, 4], BF16, name="h_bf%d" % c, tag="h_bf%d" % c, align_bytes=64) for c in range(E // 2)]
+        h_word = [held([P, 2 * C], U32, "h_word%d" % c) for c in range(E // 2)]
+        h_byte = [held([P, 2 * C], U8, "h_byte%d" % c) for c in range(E // 2)]
 
         def first_layer(e):
-            acc = bank([P, H], "acc", "acc%d" % (e % 3))
+            acc = acc_bank[e % 4]
             words, bytes_run = run_of(W1_WORD_RUNS, e), run_of(W1_BYTE_RUNS, e)
             for o in range(PASSES):
                 run = run_of(WORD_RUNS[o], e)
@@ -148,64 +146,90 @@ def tile_moe_pkd_mlp_relu_kernel(tc, x_words, x_scales, w1_words, w1_scales, w2_
                     start=(o == 0),
                     stop=(o == PASSES - 1),
                 )
-            by_slot[e] = held([P, 2, P, 2], BF16, "by_slot%d" % e)
-            sums = acc[:].rearrange("j (p u d) -> j u p d", u=2, d=2)
-            if e in RELU_ON_VECTOR:
-                nc.vector.tensor_scalar_max(by_slot[e][:], sums, 0.0)
-            else:
-                nc.scalar.activation(out=by_slot[e][:], in_=sums, func=RELU)
+            nc.scalar.activation(out=by_slot[e][:], in_=acc[:].rearrange("j (p u d) -> j u p d", u=2, d=2), func=RELU)
 
         def turn(e):
-            turned = bank([P, 2, C], "turned", "turn%d" % (e % 2))
             pairs = by_slot[e][:].rearrange("j u p d -> j (u p d)").bitcast(F32)
             for u in range(2):
-                nc.tensor.transpose(turned[:, u, :], pairs[:, u * P : (u + 1) * P], ident[:])
-            dst, src = h_bf[e // 2][:, e % 2].bitcast(F32), turned[:].rearrange("p u j -> p j u")
-            if e in TURN_ON_VECTOR:
-                nc.vector.tensor_copy(out=dst, in_=src)
-            else:
-                nc.scalar.copy(out=dst, in_=src)
+                nc.tensor.transpose(turn_bank[e % 2][:, u * C : (u + 1) * C], pairs[:, u * P : (u + 1) * P], ident[:])
+
+        def interleave(e):
+            turned = turn_bank[e % 2][:, 0 : 2 * C].rearrange("p (u j) -> p j u", u=2)
+            nc.scalar.copy(out=h_bf[e // 2][:, e % 2].bitcast(F32), in_=turned)
 
         def quantise(c):
-            parts = [(0, 1), (1, 2)] if c == 0 and False else [(0, 2)]
-            for a, b in parts:
-                words = held([P, (b - a) * C], U32, "h_word%d_%d" % (c, a), CODE_SLOTS[c] if b == 2 else "")
-                scales = held([P, (b - a) * C], U8, "h_byte%d_%d" % (c, a))
-                nc.vector.quantize_mx(out=words[:].bitcast(FP8X4), scales=scales[:], in_=h_bf[c][:, a:b].rearrange("p m j t -> p (m j t)"))
-                for m in range(a, b):
-                    h_word[2 * c + m] = words[:, (m - a) * C : (m - a + 1) * C]
-                    h_byte[2 * c + m] = scales[:, (m - a) * C : (m - a + 1) * C]
+            nc.vector.quantize_mx(out=h_word[c][:].bitcast(FP8X4), scales=h_byte[c][:], in_=h_bf[c][:].rearrange("p m j t -> p (m j t)"))
 
-        def second_layer(c, v, tag):
-            y = bank([P, 2, C], "y", tag)
+        def second_layer(c, v, sums):
             for m in range(2):
                 e = 2 * c + m
-                words, bytes_run = run_of(W2_WORD_RUNS, e), run_of(W2_BYTE_RUNS, e)
+                words = run_of(W2_WORD_RUNS, e)
                 nc.tensor.matmul_mx(
-                    out=y[:, m, :],
+                    out=sums[:, m * C : (m + 1) * C],
                     lhsT=w2_word[words][:, e - words[0], v * P // 2 : (v + 1) * P // 2].bitcast(FP4X4),
-                    lhsT_scale=w2_byte[bytes_run][:, e - bytes_run[0], v * P // 4 : (v + 1) * P // 4].bitcast(U8),
-                    rhs=h_word[e].bitcast(FP8X4),
-                    rhs_scale=h_byte[e],
+                    lhsT_scale=w2_byte[:, e, v * P // 4 : (v + 1) * P // 4].bitcast(U8),
+                    rhs=h_word[c][:, m * C : (m + 1) * C].bitcast(FP8X4),
+                    rhs_scale=h_byte[c][:, m * C : (m + 1) * C],
                     start=True,
                     stop=True,
                 )
-            y_sb = held([P, 2 * C], F32, "y_sb%d_%d" % (c, v))
-            if (c, v) in Y_ON_VECTOR:
-                nc.vector.tensor_copy(out=y_sb[:], in_=y[:].rearrange("p m j -> p (m j)"))
-            else:
-                nc.scalar.copy(out=y_sb[:], in_=y[:].rearrange("p m j -> p (m j)"))
-            gate_cols = gate_sb[c // 2][:, 2 * C * (c % 2) : 2 * C * (c % 2 + 1)]
-            nc.vector.tensor_tensor(out=window[v][:].indirect(slots_of((2 * c, 2 * c + 2))), in0=y_sb[:], in1=gate_cols, op=MULT)
-            if c == E // 2 - 1:
-                nc.sync.dma_start(out=out[v * P : (v + 1) * P, :], in_=window[v][:])
 
-        for step in STAGES:
-            if step[0] == "f":
-                first_layer(step[1])
-            elif step[0] == "t":
-                turn(step[1])
-            elif step[0] == "q":
-                quantise(step[1])
-            else:
-                second_layer(step[1], step[2], step[3])
+        y_sb = {key: held([P, (key[0][1] - key[0][0]) * C], F32, "y_sb%d_%d" % (key[0][0], key[1])) for key in SCATTERS}
+
+        def unload(c, v, sums):
+            run = run_of([key[0] for key in SCATTERS if key[1] == v], 2 * c)
+            a = (2 * c - run[0]) * C
+            nc.scalar.copy(out=y_sb[run, v][:, a : a + 2 * C], in_=sums)
+
+        def scatter(run, v):
+            gates = run_of(GATE_RUNS, run[0])
+            gate_cols = gate_sb[gates][:, (run[0] - gates[0]) * C : (run[1] - gates[0]) * C]
+            nc.vector.tensor_tensor(out=window[v][:].indirect(slots_of(run)), in0=y_sb[run, v][:], in1=gate_cols, op=MULT)
+
+        spare = [bank[:, 2 * C : 4 * C] for bank in turn_bank]
+
+        def rows(c, v, sums):
+            second_layer(c, v, sums)
+            unload(c, v, sums)
+
+        def last_of_pair(c, v):
+            turn(2 * c + 3)
+            second_layer(c, v, spare[1])
+            interleave(2 * c + 3)
+            quantise(c + 1)
+            unload(c, v, spare[1])
+            scatter((2 * c, 2 * c + 2), v)
+
+        first_layer(0)
+        first_layer(1)
+        for e in range(2):
+            turn(e)
+            interleave(e)
+        quantise(0)
+        gather_words(1, (4, 8), T, "h_bf0")
+        first_layer(2)
+        rows(0, 0, spare[0])
+        scatter((0, 2), 0)
+        first_layer(3)
+        turn(2)
+        interleave(2)
+        last_of_pair(0, 1)
+        first_layer(4)
+        first_layer(5)
+        rows(1, 0, y_bank[0][:, 0 : 2 * C])
+        scatter((2, 4), 0)
+        turn(4)
+        interleave(4)
+        last_of_pair(1, 1)
+        first_layer(6)
+        first_layer(7)
+        turn(6)
+        interleave(6)
+        last_of_pair(2, 0)
+        rows(3, 0, y_bank[0][:, 0 : 2 * C])
+        scatter((6, 8), 0)
+        nc.sync.dma_start(out=out[0:P, :], in_=window[0][:])
+        rows(2, 1, spare[0])
+        rows(3, 1, y_bank[1][:, 0 : 2 * C])
+        scatter((4, 8), 1)
+        nc.sync.dma_start(out=out[P : 2 * P, :], in_=window[1][:])

@@ -22,11 +22,11 @@ PASSES = K // 512
 BANK = 512
 CLEAR = 512
 SHIFT = 16
-WORD_RUNS = [[(0, 4), (4, 8)], [(0, 2), (2, 4), (4, 8)]]
-W1_WORD_RUNS = [(0, 1), (1, 2), (2, 3), (3, 4), (4, 6), (6, 8)]
+WORD_RUNS = [[(0, 2), (2, 8)], [(0, 2), (2, 4), (4, 8)]]
+W1_WORD_RUNS = [(e, e + 1) for e in range(E)]
 W1_BYTE_RUNS = [(0, 2), (2, 4), (4, 8)]
 W2_WORD_RUNS = [(0, 2), (2, 4), (4, 8)]
-GATE_RUNS = [(0, 2), (2, 4), (4, 8)]
+WARM = 3
 SCATTERS = [((0, 2), 0), ((0, 2), 1), ((2, 4), 0), ((2, 4), 1), ((4, 6), 0), ((6, 8), 0), ((4, 8), 1)]
 
 
@@ -44,14 +44,15 @@ def tile_moe_pkd_mlp_relu_kernel(tc, x_words, x_scales, w1_words, w1_scales, w2_
             return keep.tile(shape, dtype, name=name, align_bytes=64)
 
         offsets = keep.tile([P, E * C // 16], U16, name="offsets")
-        x_word = held([P, PASSES * T], I32, "x_word")
+        x_word = [held([P, T], I32, "x_word%d" % o) for o in range(PASSES)]
         x_byte = held([P, T // 4], I32, "x_byte")
         w1_word = {run: held([P, PASSES * (run[1] - run[0]), H // 2], I32, "w1_word%d" % run[0]) for run in W1_WORD_RUNS}
         w1_byte = {run: held([P, PASSES * (run[1] - run[0]), H // 4], I32, "w1_byte%d" % run[0]) for run in W1_BYTE_RUNS}
         w2_word = {run: held([P, run[1] - run[0], N // 2], I32, "w2_word%d" % run[0]) for run in W2_WORD_RUNS}
         w2_byte = held([P, E, N // 4], I32, "w2_byte")
         g_byte = [held([P, E * C], U8, "g_byte0"), held([P, E * C // 4], I32, "g_byte1")]
-        gate_sb = {run: held([P, (run[1] - run[0]) * C], F32, "gate_sb%d" % run[0]) for run in GATE_RUNS}
+        gate_col = held([P, 8], F32, "gate_col")
+        gate_sb = held([P, P, 8], F32, "gate_sb")
         window = [held([P, T], F32, "window%d" % v) for v in range(2)]
         zero = held([P, 8], F32, "zero")
         ident = held([P, P], F32, "ident")
@@ -59,8 +60,7 @@ def tile_moe_pkd_mlp_relu_kernel(tc, x_words, x_scales, w1_words, w1_scales, w2_
         y_bank = [psum.tile([P, BANK], F32, name="y_bank%d" % b) for b in range(2)]
         turn_bank = [psum.tile([P, BANK], F32, name="turn_bank%d" % b) for b in range(2)]
 
-        nc.gpsimd.memset(x_byte[:, 0 : T // 8], 0)
-        nc.vector.memset(x_byte[:, T // 8 : T // 4], 0)
+        nc.gpsimd.memset(x_byte[:], 0)
         nc.vector.memset(zero[:], 0.0)
         nc.vector.memset(w1_byte[0, 2][:], 0)
         nc.vector.memset(g_byte[1][:], 0)
@@ -78,74 +78,81 @@ def tile_moe_pkd_mlp_relu_kernel(tc, x_words, x_scales, w1_words, w1_scales, w2_
                 nc.sync.dma_start(out=plane[r:P:32], in_=rows[r].bitcast(I32))
 
         def load_tokens(o):
-            nc.sync.dma_start(out=x_word[:, o * T : (o + 1) * T], in_=x_words[o].rearrange("p t r -> p (t r)").bitcast(I32))
-
-        def load_gate(run):
-            nc.sync.dma_start(out=gate_sb[run][:], in_=gate[0:P, C * run[0] : C * run[1]])
+            nc.sync.dma_start(out=x_word[o][:], in_=x_words[o].rearrange("p t r -> p (t r)").bitcast(I32))
 
         def slots_of(run):
             return offsets[:, run[0] * C // 16 : run[1] * C // 16]
 
+        def load_w1(e):
+            load_words(w1_word[e, e + 1], w1_words, (e, e + 1))
+
         nc.sync.dma_start(offsets[:], offs)
+        load_w1(0)
         token_rows = x_scales.rearrange("o (q r) t -> r q o t", r=4)
         for r in range(4):
             nc.sync.dma_start(out=x_byte[r:P:SHIFT, :], in_=token_rows[r].bitcast(I32))
+        nc.sync.dma_start(out=gate_col[:], in_=gate[0].rearrange("(j c) -> j c", c=8))
         load_tokens(0)
         nc.vector.tensor_copy(out=g_byte[0][:], in_=x_byte[:].bitcast(U8).indirect(offsets[:]))
         load_scales(w1_byte[0, 2], w1_scales, (0, 2))
         load_tokens(1)
-        load_words(w1_word[0, 1], w1_words, (0, 1))
         nc.sync.dma_start(out=g_byte[1][0 : P - SHIFT, :], in_=g_byte[0][SHIFT:P, :].bitcast(I32))
-        load_words(w1_word[1, 2], w1_words, (1, 2))
+        load_w1(1)
         load_scales(w1_byte[2, 4], w1_scales, (2, 4))
-        load_words(w1_word[2, 3], w1_words, (2, 3))
+        load_w1(2)
         load_scales(w2_byte, w2_scales, (0, E))
         load_words(w2_word[0, 2], w2_words, (0, 2))
-        load_words(w1_word[3, 4], w1_words, (3, 4))
-        load_gate((0, 2))
+        load_w1(3)
         load_scales(w1_byte[4, 8], w1_scales, (4, 8))
-        load_words(w1_word[4, 6], w1_words, (4, 6))
+        load_w1(4)
+        load_w1(5)
         load_words(w2_word[2, 4], w2_words, (2, 4))
-        load_gate((2, 4))
-        load_words(w1_word[6, 8], w1_words, (6, 8))
+        load_w1(6)
+        load_w1(7)
         load_words(w2_word[4, 8], w2_words, (4, 8))
-        load_gate((4, 8))
         token_scale = [g_byte[0][:], g_byte[1][:].bitcast(U8)]
 
         g_word = {}
-
-        def gather_words(o, run, columns, tag):
-            g_word[o, run] = keep.tile([P, (run[1] - run[0]) * C], U32, name="g_word%d_%d" % (o, run[0]), tag=tag, align_bytes=64)
-            nc.vector.tensor_copy(out=g_word[o, run][:], in_=x_word[:, o * T : o * T + columns].bitcast(U32).indirect(slots_of(run)))
-
-        gather_words(0, (0, 4), T, "g_a")
-        gather_words(1, (0, 2), T, "g_b")
-        gather_words(1, (2, 4), T, "g_c")
-        gather_words(0, (4, 8), PASSES * T, "g_d")
+        for o in range(PASSES):
+            for run in WORD_RUNS[o]:
+                g_word[o, run] = held([P, (run[1] - run[0]) * C], U32, "g_word%d_%d" % (o, run[0]))
+                nc.vector.tensor_copy(out=g_word[o, run][:], in_=x_word[o][:].bitcast(U32).indirect(slots_of(run)))
 
         for v in range(2):
             for a in range(0, T, CLEAR):
                 nc.scalar.activation(out=window[v][:, a : a + CLEAR], in_=zero[:, 0:1].to_broadcast([P, CLEAR]), func=RELU)
+
+        for half in range(2):
+            for c in range(4):
+                column = gate_col[:, 4 * half + c : 4 * half + c + 1].to_broadcast([P, P])
+                nc.tensor.transpose(y_bank[half][:, c * P : (c + 1) * P], column, ident[:])
+            nc.scalar.copy(out=gate_sb[:, :, 4 * half : 4 * half + 4], in_=y_bank[half][:].rearrange("p (c j) -> p j c", c=4))
 
         by_slot = [held([P, 2, P, 2], BF16, "by_slot%d" % e) for e in range(E)]
         h_bf = [keep.tile([P, 2, C, 4], BF16, name="h_bf%d" % c, tag="h_bf%d" % c, align_bytes=64) for c in range(E // 2)]
         h_word = [held([P, 2 * C], U32, "h_word%d" % c) for c in range(E // 2)]
         h_byte = [held([P, 2 * C], U8, "h_byte%d" % c) for c in range(E // 2)]
 
+        def first_pass(e, o, acc, start, stop):
+            words, bytes_run = run_of(W1_WORD_RUNS, e), run_of(W1_BYTE_RUNS, e)
+            run = run_of(WORD_RUNS[o], e)
+            nc.tensor.matmul_mx(
+                out=acc[:],
+                lhsT=g_word[o, run][:, (e - run[0]) * C : (e - run[0] + 1) * C].bitcast(FP8X4),
+                lhsT_scale=token_scale[o][:, e * C : (e + 1) * C],
+                rhs=w1_word[words][:, PASSES * (e - words[0]) + o, :].bitcast(FP4X4),
+                rhs_scale=w1_byte[bytes_run][:, PASSES * (e - bytes_run[0]) + o, :].bitcast(U8),
+                start=start,
+                stop=stop,
+            )
+
         def first_layer(e):
             acc = acc_bank[e % 4]
-            words, bytes_run = run_of(W1_WORD_RUNS, e), run_of(W1_BYTE_RUNS, e)
             for o in range(PASSES):
-                run = run_of(WORD_RUNS[o], e)
-                nc.tensor.matmul_mx(
-                    out=acc[:],
-                    lhsT=g_word[o, run][:, (e - run[0]) * C : (e - run[0] + 1) * C].bitcast(FP8X4),
-                    lhsT_scale=token_scale[o][:, e * C : (e + 1) * C],
-                    rhs=w1_word[words][:, PASSES * (e - words[0]) + o, :].bitcast(FP4X4),
-                    rhs_scale=w1_byte[bytes_run][:, PASSES * (e - bytes_run[0]) + o, :].bitcast(U8),
-                    start=(o == 0),
-                    stop=(o == PASSES - 1),
-                )
+                first_pass(e, o, acc, o == 0, o == PASSES - 1)
+                if e == 0 and o == 0:
+                    for w in range(WARM):
+                        first_pass(0, 0, acc_bank[3], True, True)
             nc.scalar.activation(out=by_slot[e][:], in_=acc[:].rearrange("j (p u d) -> j u p d", u=2, d=2), func=RELU)
 
         def turn(e):
@@ -182,8 +189,7 @@ def tile_moe_pkd_mlp_relu_kernel(tc, x_words, x_scales, w1_words, w1_scales, w2_
             nc.scalar.copy(out=y_sb[run, v][:, a : a + 2 * C], in_=sums)
 
         def scatter(run, v):
-            gates = run_of(GATE_RUNS, run[0])
-            gate_cols = gate_sb[gates][:, (run[0] - gates[0]) * C : (run[1] - gates[0]) * C]
+            gate_cols = gate_sb[:].rearrange("p j c -> p (j c)")[:, run[0] * C : run[1] * C]
             nc.vector.tensor_tensor(out=window[v][:].indirect(slots_of(run)), in0=y_sb[run, v][:], in1=gate_cols, op=MULT)
 
         spare = [bank[:, 2 * C : 4 * C] for bank in turn_bank]
@@ -206,7 +212,6 @@ def tile_moe_pkd_mlp_relu_kernel(tc, x_words, x_scales, w1_words, w1_scales, w2_
             turn(e)
             interleave(e)
         quantise(0)
-        gather_words(1, (4, 8), T, "h_bf0")
         first_layer(2)
         rows(0, 0, spare[0])
         scatter((0, 2), 0)

@@ -25,8 +25,10 @@ SHIFT = 16
 WORD_RUNS = [[(0, 2), (2, 8)], [(0, 2), (2, 4), (4, 8)]]
 W1_WORD_RUNS = [(e, e + 1) for e in range(E)]
 W1_BYTE_RUNS = [(0, 2), (2, 4), (4, 8)]
+W2_BYTE_RUNS = [(0, 4), (4, 8)]
 W2_WORD_RUNS = [(0, 2), (2, 4), (4, 8)]
 WARM = 3
+ACC = [0, 1, 0, 1, 2, 3, 0, 1]
 SCATTERS = [((0, 2), 0), ((0, 2), 1), ((2, 4), 0), ((2, 4), 1), ((4, 6), 0), ((6, 8), 0), ((4, 8), 1)]
 
 
@@ -49,7 +51,7 @@ def tile_moe_pkd_mlp_relu_kernel(tc, x_words, x_scales, w1_words, w1_scales, w2_
         w1_word = {run: held([P, PASSES * (run[1] - run[0]), H // 2], I32, "w1_word%d" % run[0]) for run in W1_WORD_RUNS}
         w1_byte = {run: held([P, PASSES * (run[1] - run[0]), H // 4], I32, "w1_byte%d" % run[0]) for run in W1_BYTE_RUNS}
         w2_word = {run: held([P, run[1] - run[0], N // 2], I32, "w2_word%d" % run[0]) for run in W2_WORD_RUNS}
-        w2_byte = held([P, E, N // 4], I32, "w2_byte")
+        w2_byte = {run: held([P, run[1] - run[0], N // 4], I32, "w2_byte%d" % run[0]) for run in W2_BYTE_RUNS}
         g_byte = [held([P, E * C], U8, "g_byte0"), held([P, E * C // 4], I32, "g_byte1")]
         gate_col = held([P, 8], F32, "gate_col")
         gate_sb = held([P, P, 8], F32, "gate_sb")
@@ -65,9 +67,10 @@ def tile_moe_pkd_mlp_relu_kernel(tc, x_words, x_scales, w1_words, w1_scales, w2_
         nc.vector.memset(w1_byte[0, 2][:], 0)
         nc.vector.memset(g_byte[1][:], 0)
         nc.vector.memset(w1_byte[2, 4][:], 0)
-        nc.vector.memset(w2_byte[:], 0)
+        nc.vector.memset(w2_byte[0, 4][:], 0)
+        nc.vector.memset(w1_byte[4, 8][:], 0)
+        nc.vector.memset(w2_byte[4, 8][:], 0)
         make_identity(nc, ident[:])
-        nc.gpsimd.memset(w1_byte[4, 8][:], 0)
 
         def load_words(tile, words, run):
             nc.sync.dma_start(out=tile[:], in_=words[run[0] : run[1]].rearrange("e s p b -> p (e s) b").bitcast(I32))
@@ -100,15 +103,16 @@ def tile_moe_pkd_mlp_relu_kernel(tc, x_words, x_scales, w1_words, w1_scales, w2_
         load_w1(1)
         load_scales(w1_byte[2, 4], w1_scales, (2, 4))
         load_w1(2)
-        load_scales(w2_byte, w2_scales, (0, E))
-        load_words(w2_word[0, 2], w2_words, (0, 2))
         load_w1(3)
+        load_scales(w2_byte[0, 4], w2_scales, (0, 4))
+        load_words(w2_word[0, 2], w2_words, (0, 2))
         load_scales(w1_byte[4, 8], w1_scales, (4, 8))
         load_w1(4)
         load_w1(5)
         load_words(w2_word[2, 4], w2_words, (2, 4))
         load_w1(6)
         load_w1(7)
+        load_scales(w2_byte[4, 8], w2_scales, (4, 8))
         load_words(w2_word[4, 8], w2_words, (4, 8))
         token_scale = [g_byte[0][:], g_byte[1][:].bitcast(U8)]
 
@@ -129,6 +133,7 @@ def tile_moe_pkd_mlp_relu_kernel(tc, x_words, x_scales, w1_words, w1_scales, w2_
             nc.scalar.copy(out=gate_sb[:, :, 4 * half : 4 * half + 4], in_=y_bank[half][:].rearrange("p (c j) -> p j c", c=4))
 
         by_slot = [held([P, 2, P, 2], BF16, "by_slot%d" % e) for e in range(E)]
+        by_slot[2] = by_slot[1]
         h_bf = [keep.tile([P, 2, C, 4], BF16, name="h_bf%d" % c, tag="h_bf%d" % c, align_bytes=64) for c in range(E // 2)]
         h_word = [held([P, 2 * C], U32, "h_word%d" % c) for c in range(E // 2)]
         h_byte = [held([P, 2 * C], U8, "h_byte%d" % c) for c in range(E // 2)]
@@ -147,7 +152,7 @@ def tile_moe_pkd_mlp_relu_kernel(tc, x_words, x_scales, w1_words, w1_scales, w2_
             )
 
         def first_layer(e):
-            acc = acc_bank[e % 4]
+            acc = acc_bank[ACC[e]]
             for o in range(PASSES):
                 first_pass(e, o, acc, o == 0, o == PASSES - 1)
                 if e == 0 and o == 0:
@@ -155,14 +160,13 @@ def tile_moe_pkd_mlp_relu_kernel(tc, x_words, x_scales, w1_words, w1_scales, w2_
                         first_pass(0, 0, acc_bank[3], True, True)
             nc.scalar.activation(out=by_slot[e][:], in_=acc[:].rearrange("j (p u d) -> j u p d", u=2, d=2), func=RELU)
 
-        def turn(e):
+        def turn(e, turned):
             pairs = by_slot[e][:].rearrange("j u p d -> j (u p d)").bitcast(F32)
             for u in range(2):
-                nc.tensor.transpose(turn_bank[e % 2][:, u * C : (u + 1) * C], pairs[:, u * P : (u + 1) * P], ident[:])
+                nc.tensor.transpose(turned[:, u * C : (u + 1) * C], pairs[:, u * P : (u + 1) * P], ident[:])
 
-        def interleave(e):
-            turned = turn_bank[e % 2][:, 0 : 2 * C].rearrange("p (u j) -> p j u", u=2)
-            nc.scalar.copy(out=h_bf[e // 2][:, e % 2].bitcast(F32), in_=turned)
+        def interleave(e, turned):
+            nc.scalar.copy(out=h_bf[e // 2][:, e % 2].bitcast(F32), in_=turned.rearrange("p (u j) -> p j u", u=2))
 
         def quantise(c):
             nc.vector.quantize_mx(out=h_word[c][:].bitcast(FP8X4), scales=h_byte[c][:], in_=h_bf[c][:].rearrange("p m j t -> p (m j t)"))
@@ -170,71 +174,87 @@ def tile_moe_pkd_mlp_relu_kernel(tc, x_words, x_scales, w1_words, w1_scales, w2_
         def second_layer(c, v, sums):
             for m in range(2):
                 e = 2 * c + m
-                words = run_of(W2_WORD_RUNS, e)
+                words, bytes_run = run_of(W2_WORD_RUNS, e), run_of(W2_BYTE_RUNS, e)
                 nc.tensor.matmul_mx(
                     out=sums[:, m * C : (m + 1) * C],
                     lhsT=w2_word[words][:, e - words[0], v * P // 2 : (v + 1) * P // 2].bitcast(FP4X4),
-                    lhsT_scale=w2_byte[:, e, v * P // 4 : (v + 1) * P // 4].bitcast(U8),
+                    lhsT_scale=w2_byte[bytes_run][:, e - bytes_run[0], v * P // 4 : (v + 1) * P // 4].bitcast(U8),
                     rhs=h_word[c][:, m * C : (m + 1) * C].bitcast(FP8X4),
                     rhs_scale=h_byte[c][:, m * C : (m + 1) * C],
                     start=True,
                     stop=True,
                 )
 
-        y_sb = {key: held([P, (key[0][1] - key[0][0]) * C], F32, "y_sb%d_%d" % (key[0][0], key[1])) for key in SCATTERS}
+        y_tile = {key: held([P, (key[0][1] - key[0][0]) * C], F32, "y_sb%d_%d" % (key[0][0], key[1])) for key in SCATTERS}
+        y_sb = {key: y_tile[key][:] for key in SCATTERS}
+        for c in range(2):
+            y_sb[(2 * c, 2 * c + 2), 1] = by_slot[2 * c + 3][:].rearrange("j u p d -> j (u p d)").bitcast(F32)
 
         def unload(c, v, sums):
             run = run_of([key[0] for key in SCATTERS if key[1] == v], 2 * c)
             a = (2 * c - run[0]) * C
-            nc.scalar.copy(out=y_sb[run, v][:, a : a + 2 * C], in_=sums)
+            if (c, v) == (0, 0):
+                nc.vector.tensor_copy(out=y_sb[run, v][:, a : a + 2 * C], in_=sums)
+            else:
+                nc.scalar.copy(out=y_sb[run, v][:, a : a + 2 * C], in_=sums)
 
         def scatter(run, v):
             gate_cols = gate_sb[:].rearrange("p j c -> p (j c)")[:, run[0] * C : run[1] * C]
-            nc.vector.tensor_tensor(out=window[v][:].indirect(slots_of(run)), in0=y_sb[run, v][:], in1=gate_cols, op=MULT)
+            nc.vector.tensor_tensor(out=window[v][:].indirect(slots_of(run)), in0=y_sb[run, v], in1=gate_cols, op=MULT)
 
-        spare = [bank[:, 2 * C : 4 * C] for bank in turn_bank]
+        def low(bank):
+            return bank[:, 0 : 2 * C]
 
-        def rows(c, v, sums):
-            second_layer(c, v, sums)
-            unload(c, v, sums)
+        def high(bank):
+            return bank[:, 2 * C : 4 * C]
 
-        def last_of_pair(c, v):
-            turn(2 * c + 3)
-            second_layer(c, v, spare[1])
-            interleave(2 * c + 3)
-            quantise(c + 1)
-            unload(c, v, spare[1])
-            scatter((2 * c, 2 * c + 2), v)
+        def regroup(e, turned):
+            turn(e, turned)
+            interleave(e, turned)
 
         first_layer(0)
         first_layer(1)
-        for e in range(2):
-            turn(e)
-            interleave(e)
+        regroup(0, low(turn_bank[0]))
+        regroup(1, low(turn_bank[1]))
         quantise(0)
         first_layer(2)
-        rows(0, 0, spare[0])
-        scatter((0, 2), 0)
         first_layer(3)
-        turn(2)
-        interleave(2)
-        last_of_pair(0, 1)
+        second_layer(0, 0, low(y_bank[0]))
+        unload(0, 0, low(y_bank[0]))
+        scatter((0, 2), 0)
+        second_layer(0, 1, high(turn_bank[0]))
+        regroup(2, low(turn_bank[0]))
+        regroup(3, high(y_bank[0]))
+        quantise(1)
+        unload(0, 1, high(turn_bank[0]))
+        scatter((0, 2), 1)
         first_layer(4)
         first_layer(5)
-        rows(1, 0, y_bank[0][:, 0 : 2 * C])
+        second_layer(1, 0, low(acc_bank[2]))
+        unload(1, 0, low(acc_bank[2]))
         scatter((2, 4), 0)
-        turn(4)
-        interleave(4)
-        last_of_pair(1, 1)
+        second_layer(1, 1, low(acc_bank[3]))
+        regroup(4, low(turn_bank[1]))
+        regroup(5, low(turn_bank[0]))
+        quantise(2)
+        unload(1, 1, low(acc_bank[3]))
+        scatter((2, 4), 1)
         first_layer(6)
         first_layer(7)
-        turn(6)
-        interleave(6)
-        last_of_pair(2, 0)
-        rows(3, 0, y_bank[0][:, 0 : 2 * C])
+        regroup(6, low(turn_bank[1]))
+        turn(7, low(turn_bank[0]))
+        second_layer(2, 0, high(turn_bank[0]))
+        interleave(7, low(turn_bank[0]))
+        quantise(3)
+        unload(2, 0, high(turn_bank[0]))
+        scatter((4, 6), 0)
+        second_layer(3, 0, low(y_bank[0]))
+        unload(3, 0, low(y_bank[0]))
         scatter((6, 8), 0)
         nc.sync.dma_start(out=out[0:P, :], in_=window[0][:])
-        rows(2, 1, spare[0])
-        rows(3, 1, y_bank[1][:, 0 : 2 * C])
+        second_layer(2, 1, high(turn_bank[1]))
+        unload(2, 1, high(turn_bank[1]))
+        second_layer(3, 1, low(y_bank[1]))
+        unload(3, 1, low(y_bank[1]))
         scatter((4, 8), 1)
         nc.sync.dma_start(out=out[P : 2 * P, :], in_=window[1][:])

@@ -63,6 +63,7 @@ def tile_moe_pkd_mlp_relu_kernel(tc, x_words, x_scales, w1_words, w1_scales, w2_
         turn_bank = [psum.tile([P, BANK], F32, name="turn_bank%d" % b) for b in range(2)]
 
         nc.gpsimd.memset(x_byte[:], 0)
+        nc.vector.memset(ident[:], 0.0)
         nc.vector.memset(zero[:], 0.0)
         nc.vector.memset(w1_byte[0, 2][:], 0)
         nc.vector.memset(g_byte[1][:], 0)
@@ -70,7 +71,7 @@ def tile_moe_pkd_mlp_relu_kernel(tc, x_words, x_scales, w1_words, w1_scales, w2_
         nc.vector.memset(w2_byte[0, 4][:], 0)
         nc.vector.memset(w1_byte[4, 8][:], 0)
         nc.vector.memset(w2_byte[4, 8][:], 0)
-        make_identity(nc, ident[:])
+        make_identity(nc, ident[:], nomemset=True)
 
         def load_words(tile, words, run):
             nc.sync.dma_start(out=tile[:], in_=words[run[0] : run[1]].rearrange("e s p b -> p (e s) b").bitcast(I32))
@@ -158,7 +159,9 @@ def tile_moe_pkd_mlp_relu_kernel(tc, x_words, x_scales, w1_words, w1_scales, w2_
                 if e == 0 and o == 0:
                     for w in range(WARM):
                         first_pass(0, 0, acc_bank[3], True, True)
-            nc.scalar.activation(out=by_slot[e][:], in_=acc[:].rearrange("j (p u d) -> j u p d", u=2, d=2), func=RELU)
+            sums = acc[:].rearrange("j (p u d) -> j u p d", u=2, d=2)
+            for part in (slice(0, 1), slice(1, 2)) if e == 1 else (slice(0, 2),):
+                nc.scalar.activation(out=by_slot[e][:, part], in_=sums[:, part], func=RELU)
 
         def turn(e, turned):
             pairs = by_slot[e][:].rearrange("j u p d -> j (u p d)").bitcast(F32)
@@ -168,8 +171,9 @@ def tile_moe_pkd_mlp_relu_kernel(tc, x_words, x_scales, w1_words, w1_scales, w2_
         def interleave(e, turned):
             nc.scalar.copy(out=h_bf[e // 2][:, e % 2].bitcast(F32), in_=turned.rearrange("p (u j) -> p j u", u=2))
 
-        def quantise(c):
-            nc.vector.quantize_mx(out=h_word[c][:].bitcast(FP8X4), scales=h_byte[c][:], in_=h_bf[c][:].rearrange("p m j t -> p (m j t)"))
+        def quantise(c, a=0, b=2):
+            values = h_bf[c][:, a:b].rearrange("p m j t -> p (m j t)")
+            nc.vector.quantize_mx(out=h_word[c][:, a * C : b * C].bitcast(FP8X4), scales=h_byte[c][:, a * C : b * C], in_=values)
 
         def second_layer(c, v, sums):
             for m in range(2):
@@ -214,9 +218,9 @@ def tile_moe_pkd_mlp_relu_kernel(tc, x_words, x_scales, w1_words, w1_scales, w2_
 
         first_layer(0)
         first_layer(1)
-        regroup(0, low(turn_bank[0]))
-        regroup(1, low(turn_bank[1]))
-        quantise(0)
+        for e in range(2):
+            regroup(e, low(turn_bank[e]))
+            quantise(0, e, e + 1)
         first_layer(2)
         first_layer(3)
         second_layer(0, 0, low(y_bank[0]))
@@ -242,11 +246,10 @@ def tile_moe_pkd_mlp_relu_kernel(tc, x_words, x_scales, w1_words, w1_scales, w2_
         first_layer(6)
         first_layer(7)
         regroup(6, low(turn_bank[1]))
-        turn(7, low(turn_bank[0]))
-        second_layer(2, 0, high(turn_bank[0]))
-        interleave(7, low(turn_bank[0]))
+        regroup(7, low(turn_bank[0]))
         quantise(3)
-        unload(2, 0, high(turn_bank[0]))
+        second_layer(2, 0, low(acc_bank[2]))
+        unload(2, 0, low(acc_bank[2]))
         scatter((4, 6), 0)
         second_layer(3, 0, low(y_bank[0]))
         unload(3, 0, low(y_bank[0]))
@@ -257,4 +260,5 @@ def tile_moe_pkd_mlp_relu_kernel(tc, x_words, x_scales, w1_words, w1_scales, w2_
         second_layer(3, 1, low(y_bank[1]))
         unload(3, 1, low(y_bank[1]))
         scatter((4, 8), 1)
-        nc.sync.dma_start(out=out[P : 2 * P, :], in_=window[1][:])
+        nc.sync.dma_start(out=out[P : 2 * P, 0 : T // 2], in_=window[1][:, 0 : T // 2])
+        nc.scalar.dma_start(out=out[P : 2 * P, T // 2 : T], in_=window[1][:, T // 2 : T])

@@ -28,7 +28,7 @@ W1_BYTE_RUNS = [(0, 2), (2, 4), (4, 8)]
 W2_BYTE_RUNS = [(0, 4), (4, 8)]
 W2_WORD_RUNS = [(0, 2), (2, 4), (4, 8)]
 WARM = 3
-ACC = [0, 1, 0, 1, 2, 3, 0, 1]
+ACC = [0, 1, 0, 1, 2, 3, 3, 2]
 SCATTERS = [((0, 2), 0), ((0, 2), 1), ((2, 4), 0), ((2, 4), 1), ((4, 6), 0), ((6, 8), 0), ((4, 8), 1)]
 
 
@@ -234,14 +234,14 @@ def tile_moe_pkd_mlp_relu_kernel(tc, x_words, x_scales, w1_words, w1_scales, w2_
         scatter((0, 2), 1)
         first_layer(4)
         first_layer(5)
-        second_layer(1, 0, low(acc_bank[2]))
-        unload(1, 0, low(acc_bank[2]))
+        second_layer(1, 0, low(y_bank[1]))
+        unload(1, 0, low(y_bank[1]))
         scatter((2, 4), 0)
-        second_layer(1, 1, low(acc_bank[3]))
         regroup(4, low(turn_bank[1]))
         regroup(5, low(turn_bank[0]))
+        second_layer(1, 1, high(y_bank[1]))
         quantise(2)
-        unload(1, 1, low(acc_bank[3]))
+        unload(1, 1, high(y_bank[1]))
         scatter((2, 4), 1)
         first_layer(6)
         first_layer(7)
@@ -255,10 +255,10 @@ def tile_moe_pkd_mlp_relu_kernel(tc, x_words, x_scales, w1_words, w1_scales, w2_
         unload(3, 0, low(y_bank[0]))
         scatter((6, 8), 0)
         nc.sync.dma_start(out=out[0:P, :], in_=window[0][:])
-        second_layer(2, 1, high(turn_bank[1]))
-        unload(2, 1, high(turn_bank[1]))
-        second_layer(3, 1, low(y_bank[1]))
-        unload(3, 1, low(y_bank[1]))
+        second_layer(2, 1, high(acc_bank[2]))
+        unload(2, 1, high(acc_bank[2]))
+        second_layer(3, 1, low(acc_bank[0]))
+        unload(3, 1, low(acc_bank[0]))
         scatter((4, 8), 1)
         nc.sync.dma_start(out=out[P : 2 * P, 0 : T // 2], in_=window[1][:, 0 : T // 2])
         nc.scalar.dma_start(out=out[P : 2 * P, T // 2 : T], in_=window[1][:, T // 2 : T])

@@ -22,14 +22,15 @@ PASSES = K // 512
 BANK = 512
 CLEAR = 512
 SHIFT = 16
+GATE_COLS = E * C // P
+
 WORD_RUNS = [[(0, 2), (2, 8)], [(0, 2), (2, 4), (4, 8)]]
-W1_WORD_RUNS = [(e, e + 1) for e in range(E)]
 W1_BYTE_RUNS = [(0, 2), (2, 4), (4, 8)]
 W2_BYTE_RUNS = [(0, 4), (4, 8)]
 W2_WORD_RUNS = [(0, 2), (2, 4), (4, 8)]
-WARM = 3
+SCATTER_RUNS = [[(0, 2), (2, 4), (4, 6), (6, 8)], [(0, 2), (2, 4), (4, 8)]]
 ACC = [0, 1, 0, 1, 2, 3, 3, 2]
-SCATTERS = [((0, 2), 0), ((0, 2), 1), ((2, 4), 0), ((2, 4), 1), ((4, 6), 0), ((6, 8), 0), ((4, 8), 1)]
+WARM_SLOTS = [0, 2, 2]
 
 
 def run_of(runs, e):
@@ -48,13 +49,14 @@ def tile_moe_pkd_mlp_relu_kernel(tc, x_words, x_scales, w1_words, w1_scales, w2_
         offsets = keep.tile([P, E * C // 16], U16, name="offsets")
         x_word = [held([P, T], I32, "x_word%d" % o) for o in range(PASSES)]
         x_byte = held([P, T // 4], I32, "x_byte")
-        w1_word = {run: held([P, PASSES * (run[1] - run[0]), H // 2], I32, "w1_word%d" % run[0]) for run in W1_WORD_RUNS}
+        w1_word = [held([P, PASSES, H // 2], I32, "w1_word%d" % e) for e in range(E)]
         w1_byte = {run: held([P, PASSES * (run[1] - run[0]), H // 4], I32, "w1_byte%d" % run[0]) for run in W1_BYTE_RUNS}
         w2_word = {run: held([P, run[1] - run[0], N // 2], I32, "w2_word%d" % run[0]) for run in W2_WORD_RUNS}
         w2_byte = {run: held([P, run[1] - run[0], N // 4], I32, "w2_byte%d" % run[0]) for run in W2_BYTE_RUNS}
-        g_byte = [held([P, E * C], U8, "g_byte0"), held([P, E * C // 4], I32, "g_byte1")]
-        gate_col = held([P, 8], F32, "gate_col")
-        gate_sb = held([P, P, 8], F32, "gate_sb")
+        slot_byte = held([P, E * C], U8, "slot_byte")
+        moved_byte = held([P, E * C // 4], I32, "moved_byte")
+        gate_col = held([P, GATE_COLS], F32, "gate_col")
+        gate_sb = held([P, P, GATE_COLS], F32, "gate_sb")
         window = [held([P, T], F32, "window%d" % v) for v in range(2)]
         zero = held([P, 8], F32, "zero")
         ident = held([P, P], F32, "ident")
@@ -66,7 +68,7 @@ def tile_moe_pkd_mlp_relu_kernel(tc, x_words, x_scales, w1_words, w1_scales, w2_
         nc.vector.memset(ident[:], 0.0)
         nc.vector.memset(zero[:], 0.0)
         nc.vector.memset(w1_byte[0, 2][:], 0)
-        nc.vector.memset(g_byte[1][:], 0)
+        nc.vector.memset(moved_byte[:], 0)
         nc.vector.memset(w1_byte[2, 4][:], 0)
         nc.vector.memset(w2_byte[0, 4][:], 0)
         nc.vector.memset(w1_byte[4, 8][:], 0)
@@ -84,23 +86,23 @@ def tile_moe_pkd_mlp_relu_kernel(tc, x_words, x_scales, w1_words, w1_scales, w2_
         def load_tokens(o):
             nc.sync.dma_start(out=x_word[o][:], in_=x_words[o].rearrange("p t r -> p (t r)").bitcast(I32))
 
+        def load_w1(e):
+            load_words(w1_word[e], w1_words, (e, e + 1))
+
         def slots_of(run):
             return offsets[:, run[0] * C // 16 : run[1] * C // 16]
-
-        def load_w1(e):
-            load_words(w1_word[e, e + 1], w1_words, (e, e + 1))
 
         nc.sync.dma_start(offsets[:], offs)
         load_w1(0)
         token_rows = x_scales.rearrange("o (q r) t -> r q o t", r=4)
         for r in range(4):
             nc.sync.dma_start(out=x_byte[r:P:SHIFT, :], in_=token_rows[r].bitcast(I32))
-        nc.sync.dma_start(out=gate_col[:], in_=gate[0].rearrange("(j c) -> j c", c=8))
+        nc.sync.dma_start(out=gate_col[:], in_=gate[0].rearrange("(j c) -> j c", c=GATE_COLS))
         load_tokens(0)
-        nc.vector.tensor_copy(out=g_byte[0][:], in_=x_byte[:].bitcast(U8).indirect(offsets[:]))
+        nc.vector.tensor_copy(out=slot_byte[:], in_=x_byte[:].bitcast(U8).indirect(offsets[:]))
         load_scales(w1_byte[0, 2], w1_scales, (0, 2))
         load_tokens(1)
-        nc.sync.dma_start(out=g_byte[1][0 : P - SHIFT, :], in_=g_byte[0][SHIFT:P, :].bitcast(I32))
+        nc.sync.dma_start(out=moved_byte[0 : P - SHIFT, :], in_=slot_byte[SHIFT:P, :].bitcast(I32))
         load_w1(1)
         load_scales(w1_byte[2, 4], w1_scales, (2, 4))
         load_w1(2)
@@ -115,13 +117,13 @@ def tile_moe_pkd_mlp_relu_kernel(tc, x_words, x_scales, w1_words, w1_scales, w2_
         load_w1(7)
         load_scales(w2_byte[4, 8], w2_scales, (4, 8))
         load_words(w2_word[4, 8], w2_words, (4, 8))
-        token_scale = [g_byte[0][:], g_byte[1][:].bitcast(U8)]
+        slot_scale = [slot_byte[:], moved_byte[:].bitcast(U8)]
 
-        g_word = {}
+        slot_word = {}
         for o in range(PASSES):
             for run in WORD_RUNS[o]:
-                g_word[o, run] = held([P, (run[1] - run[0]) * C], U32, "g_word%d_%d" % (o, run[0]))
-                nc.vector.tensor_copy(out=g_word[o, run][:], in_=x_word[o][:].bitcast(U32).indirect(slots_of(run)))
+                slot_word[o, run] = held([P, (run[1] - run[0]) * C], U32, "slot_word%d_%d" % (o, run[0]))
+                nc.vector.tensor_copy(out=slot_word[o, run][:], in_=x_word[o][:].bitcast(U32).indirect(slots_of(run)))
 
         for v in range(2):
             for a in range(0, T, CLEAR):
@@ -133,132 +135,133 @@ def tile_moe_pkd_mlp_relu_kernel(tc, x_words, x_scales, w1_words, w1_scales, w2_
                 nc.tensor.transpose(y_bank[half][:, c * P : (c + 1) * P], column, ident[:])
             nc.scalar.copy(out=gate_sb[:, :, 4 * half : 4 * half + 4], in_=y_bank[half][:].rearrange("p (c j) -> p j c", c=4))
 
-        by_slot = [held([P, 2, P, 2], BF16, "by_slot%d" % e) for e in range(E)]
+        by_slot = {e: held([P, 2, P, 2], BF16, "by_slot%d" % e) for e in range(E) if e != 2}
         by_slot[2] = by_slot[1]
-        h_bf = [keep.tile([P, 2, C, 4], BF16, name="h_bf%d" % c, tag="h_bf%d" % c, align_bytes=64) for c in range(E // 2)]
+        h_bf = [held([P, 2, C, 4], BF16, "h_bf%d" % c) for c in range(E // 2)]
         h_word = [held([P, 2 * C], U32, "h_word%d" % c) for c in range(E // 2)]
         h_byte = [held([P, 2 * C], U8, "h_byte%d" % c) for c in range(E // 2)]
 
-        def first_pass(e, o, acc, start, stop):
-            words, bytes_run = run_of(W1_WORD_RUNS, e), run_of(W1_BYTE_RUNS, e)
-            run = run_of(WORD_RUNS[o], e)
+        def as_words(e):
+            return by_slot[e][:].rearrange("j u p d -> j (u p d)").bitcast(F32)
+
+        def first_pass(slots, e, o, acc, start, stop):
+            words, scales = run_of(WORD_RUNS[o], slots), run_of(W1_BYTE_RUNS, e)
             nc.tensor.matmul_mx(
                 out=acc[:],
-                lhsT=g_word[o, run][:, (e - run[0]) * C : (e - run[0] + 1) * C].bitcast(FP8X4),
-                lhsT_scale=token_scale[o][:, e * C : (e + 1) * C],
-                rhs=w1_word[words][:, PASSES * (e - words[0]) + o, :].bitcast(FP4X4),
-                rhs_scale=w1_byte[bytes_run][:, PASSES * (e - bytes_run[0]) + o, :].bitcast(U8),
+                lhsT=slot_word[o, words][:, (slots - words[0]) * C : (slots - words[0] + 1) * C].bitcast(FP8X4),
+                lhsT_scale=slot_scale[o][:, slots * C : (slots + 1) * C],
+                rhs=w1_word[e][:, o, :].bitcast(FP4X4),
+                rhs_scale=w1_byte[scales][:, PASSES * (e - scales[0]) + o, :].bitcast(U8),
                 start=start,
                 stop=stop,
             )
 
-        def first_layer(e):
-            acc = acc_bank[ACC[e]]
+        def relu(e, halves=slice(0, 2)):
+            sums = acc_bank[ACC[e]][:].rearrange("j (p u d) -> j u p d", u=2, d=2)
+            nc.scalar.activation(out=by_slot[e][:, halves], in_=sums[:, halves], func=RELU)
+
+        def first_products(e):
             for o in range(PASSES):
-                first_pass(e, o, acc, o == 0, o == PASSES - 1)
-                if e == 0 and o == 0:
-                    for w in range(WARM):
-                        first_pass(0, 0, acc_bank[3], True, True)
-            sums = acc[:].rearrange("j (p u d) -> j u p d", u=2, d=2)
-            for part in (slice(0, 1), slice(1, 2)) if e == 1 else (slice(0, 2),):
-                nc.scalar.activation(out=by_slot[e][:, part], in_=sums[:, part], func=RELU)
+                first_pass(e, e, o, acc_bank[ACC[e]], o == 0, o == PASSES - 1)
 
-        def turn(e, turned):
-            pairs = by_slot[e][:].rearrange("j u p d -> j (u p d)").bitcast(F32)
+        def first_layer(e):
+            first_products(e)
+            relu(e)
+
+        def regroup(e, turned):
             for u in range(2):
-                nc.tensor.transpose(turned[:, u * C : (u + 1) * C], pairs[:, u * P : (u + 1) * P], ident[:])
-
-        def interleave(e, turned):
+                nc.tensor.transpose(turned[:, u * C : (u + 1) * C], as_words(e)[:, u * P : (u + 1) * P], ident[:])
             nc.scalar.copy(out=h_bf[e // 2][:, e % 2].bitcast(F32), in_=turned.rearrange("p (u j) -> p j u", u=2))
 
         def quantise(c, a=0, b=2):
             values = h_bf[c][:, a:b].rearrange("p m j t -> p (m j t)")
             nc.vector.quantize_mx(out=h_word[c][:, a * C : b * C].bitcast(FP8X4), scales=h_byte[c][:, a * C : b * C], in_=values)
 
-        def second_layer(c, v, sums):
+        def second_products(c, v, sums):
             for m in range(2):
                 e = 2 * c + m
-                words, bytes_run = run_of(W2_WORD_RUNS, e), run_of(W2_BYTE_RUNS, e)
+                words, scales = run_of(W2_WORD_RUNS, e), run_of(W2_BYTE_RUNS, e)
                 nc.tensor.matmul_mx(
                     out=sums[:, m * C : (m + 1) * C],
                     lhsT=w2_word[words][:, e - words[0], v * P // 2 : (v + 1) * P // 2].bitcast(FP4X4),
-                    lhsT_scale=w2_byte[bytes_run][:, e - bytes_run[0], v * P // 4 : (v + 1) * P // 4].bitcast(U8),
+                    lhsT_scale=w2_byte[scales][:, e - scales[0], v * P // 4 : (v + 1) * P // 4].bitcast(U8),
                     rhs=h_word[c][:, m * C : (m + 1) * C].bitcast(FP8X4),
                     rhs_scale=h_byte[c][:, m * C : (m + 1) * C],
                     start=True,
                     stop=True,
                 )
 
-        y_tile = {key: held([P, (key[0][1] - key[0][0]) * C], F32, "y_sb%d_%d" % (key[0][0], key[1])) for key in SCATTERS}
-        y_sb = {key: y_tile[key][:] for key in SCATTERS}
-        for c in range(2):
-            y_sb[(2 * c, 2 * c + 2), 1] = by_slot[2 * c + 3][:].rearrange("j u p d -> j (u p d)").bitcast(F32)
+        y_sb = {((2 * c, 2 * c + 2), 1): as_words(2 * c + 3) for c in range(2)}
+        for v in range(2):
+            for run in SCATTER_RUNS[v]:
+                if (run, v) not in y_sb:
+                    y_sb[run, v] = held([P, (run[1] - run[0]) * C], F32, "y_sb%d_%d" % (run[0], v))[:]
 
-        def unload(c, v, sums):
-            run = run_of([key[0] for key in SCATTERS if key[1] == v], 2 * c)
-            a = (2 * c - run[0]) * C
-            if (c, v) == (0, 0):
-                nc.vector.tensor_copy(out=y_sb[run, v][:, a : a + 2 * C], in_=sums)
-            else:
-                nc.scalar.copy(out=y_sb[run, v][:, a : a + 2 * C], in_=sums)
+        def y_of(c, v):
+            run = run_of(SCATTER_RUNS[v], 2 * c)
+            return y_sb[run, v][:, (2 * c - run[0]) * C : (2 * c + 2 - run[0]) * C]
+
+        def second_layer(c, v, sums):
+            second_products(c, v, sums)
+            nc.scalar.copy(out=y_of(c, v), in_=sums)
 
         def scatter(run, v):
             gate_cols = gate_sb[:].rearrange("p j c -> p (j c)")[:, run[0] * C : run[1] * C]
             nc.vector.tensor_tensor(out=window[v][:].indirect(slots_of(run)), in0=y_sb[run, v], in1=gate_cols, op=MULT)
 
         def low(bank):
-            return bank[:, 0 : 2 * C]
+            return bank[:, 0 : BANK // 2]
 
         def high(bank):
-            return bank[:, 2 * C : 4 * C]
+            return bank[:, BANK // 2 : BANK]
 
-        def regroup(e, turned):
-            turn(e, turned)
-            interleave(e, turned)
-
-        first_layer(0)
-        first_layer(1)
+        first_pass(0, 0, 0, acc_bank[ACC[0]], True, False)
+        for slots in WARM_SLOTS:
+            first_pass(slots, 0, 0, acc_bank[3], True, True)
+        first_pass(0, 0, 1, acc_bank[ACC[0]], False, True)
+        relu(0)
+        first_products(1)
+        for u in range(2):
+            relu(1, slice(u, u + 1))
         for e in range(2):
             regroup(e, low(turn_bank[e]))
             quantise(0, e, e + 1)
+
         first_layer(2)
         first_layer(3)
-        second_layer(0, 0, low(y_bank[0]))
-        unload(0, 0, low(y_bank[0]))
+        second_products(0, 0, low(y_bank[0]))
+        nc.vector.tensor_copy(out=y_of(0, 0), in_=low(y_bank[0]))
         scatter((0, 2), 0)
-        second_layer(0, 1, high(turn_bank[0]))
+        second_products(0, 1, high(turn_bank[0]))
         regroup(2, low(turn_bank[0]))
         regroup(3, high(y_bank[0]))
         quantise(1)
-        unload(0, 1, high(turn_bank[0]))
+        nc.scalar.copy(out=y_of(0, 1), in_=high(turn_bank[0]))
         scatter((0, 2), 1)
+
         first_layer(4)
         first_layer(5)
         second_layer(1, 0, low(y_bank[1]))
-        unload(1, 0, low(y_bank[1]))
         scatter((2, 4), 0)
         regroup(4, low(turn_bank[1]))
         regroup(5, low(turn_bank[0]))
-        second_layer(1, 1, high(y_bank[1]))
+        second_products(1, 1, high(y_bank[1]))
         quantise(2)
-        unload(1, 1, high(y_bank[1]))
+        nc.scalar.copy(out=y_of(1, 1), in_=high(y_bank[1]))
         scatter((2, 4), 1)
+
         first_layer(6)
         first_layer(7)
         regroup(6, low(turn_bank[1]))
         regroup(7, low(turn_bank[0]))
         quantise(3)
-        second_layer(2, 0, low(acc_bank[2]))
-        unload(2, 0, low(acc_bank[2]))
+        second_layer(2, 0, low(acc_bank[ACC[7]]))
         scatter((4, 6), 0)
         second_layer(3, 0, low(y_bank[0]))
-        unload(3, 0, low(y_bank[0]))
         scatter((6, 8), 0)
         nc.sync.dma_start(out=out[0:P, :], in_=window[0][:])
-        second_layer(2, 1, high(acc_bank[2]))
-        unload(2, 1, high(acc_bank[2]))
+        second_layer(2, 1, high(acc_bank[ACC[7]]))
         second_layer(3, 1, low(acc_bank[0]))
-        unload(3, 1, low(acc_bank[0]))
         scatter((4, 8), 1)
         nc.sync.dma_start(out=out[P : 2 * P, 0 : T // 2], in_=window[1][:, 0 : T // 2])
         nc.scalar.dma_start(out=out[P : 2 * P, T // 2 : T], in_=window[1][:, T // 2 : T])

@@ -15,6 +15,7 @@ U8 = mybir.dt.uint8
 FP8X4 = mybir.dt.float8_e4m3fn_x4
 FP4X4 = mybir.dt.float4_e2m1fn_x4
 RELU = mybir.ActivationFunctionType.Relu
+COPY = mybir.ActivationFunctionType.Copy
 MULT = mybir.AluOpType.mult
 
 P = 128
@@ -25,10 +26,11 @@ SHIFT = 16
 GATE_COLS = E * C // P
 
 WORD_RUNS = [[(0, 2), (2, 8)], [(0, 2), (2, 4), (4, 8)]]
-W1_BYTE_RUNS = [(0, 2), (2, 4), (4, 8)]
+W1_BYTE_RUNS = [(0, 2), (2, 4), (4, 6), (6, 8)]
 W2_BYTE_RUNS = [(0, 4), (4, 8)]
-W2_WORD_RUNS = [(0, 2), (2, 4), (4, 8)]
-SCATTER_RUNS = [[(0, 2), (2, 4), (4, 6), (6, 8)], [(0, 2), (2, 4), (4, 8)]]
+W2_WORD_RUNS = [(0, 2), (2, 4), (4, 6), (6, 8)]
+W1_WORD_RUNS = [(0, 1), (1, 2), (2, 3), (3, 4), (4, 5), (5, 6), (6, 7), (7, 8)]
+SCATTER_RUNS = [[(0, 2), (2, 4), (4, 6), (6, 8)], [(0, 2), (2, 4), (4, 6), (6, 8)]]
 ACC = [0, 1, 0, 1, 2, 3, 3, 2]
 WARM_SLOTS = [0, 2, 2]
 
@@ -43,13 +45,13 @@ def tile_moe_pkd_mlp_relu_kernel(tc, x_words, x_scales, w1_words, w1_scales, w2_
         keep = ctx.enter_context(tc.tile_pool(name="keep", bufs=1))
         psum = ctx.enter_context(tc.psum_pool(name="psum", bufs=1))
 
-        def held(shape, dtype, name):
-            return keep.tile(shape, dtype, name=name, align_bytes=64)
+        def held(shape, dtype, name, tag=""):
+            return keep.tile(shape, dtype, name=name, tag=tag, align_bytes=64)
 
         offsets = keep.tile([P, E * C // 16], U16, name="offsets")
         x_word = [held([P, T], I32, "x_word%d" % o) for o in range(PASSES)]
         x_byte = held([P, T // 4], I32, "x_byte")
-        w1_word = [held([P, PASSES, H // 2], I32, "w1_word%d" % e) for e in range(E)]
+        w1_word = {run: held([P, PASSES * (run[1] - run[0]), H // 2], I32, "w1_word%d" % run[0]) for run in W1_WORD_RUNS}
         w1_byte = {run: held([P, PASSES * (run[1] - run[0]), H // 4], I32, "w1_byte%d" % run[0]) for run in W1_BYTE_RUNS}
         w2_word = {run: held([P, run[1] - run[0], N // 2], I32, "w2_word%d" % run[0]) for run in W2_WORD_RUNS}
         w2_byte = {run: held([P, run[1] - run[0], N // 4], I32, "w2_byte%d" % run[0]) for run in W2_BYTE_RUNS}
@@ -71,7 +73,8 @@ def tile_moe_pkd_mlp_relu_kernel(tc, x_words, x_scales, w1_words, w1_scales, w2_
         nc.vector.memset(moved_byte[:], 0)
         nc.vector.memset(w1_byte[2, 4][:], 0)
         nc.vector.memset(w2_byte[0, 4][:], 0)
-        nc.vector.memset(w1_byte[4, 8][:], 0)
+        nc.vector.memset(w1_byte[4, 6][:], 0)
+        nc.vector.memset(w1_byte[6, 8][:], 0)
         nc.vector.memset(w2_byte[4, 8][:], 0)
         make_identity(nc, ident[:], nomemset=True)
 
@@ -87,7 +90,8 @@ def tile_moe_pkd_mlp_relu_kernel(tc, x_words, x_scales, w1_words, w1_scales, w2_
             nc.sync.dma_start(out=x_word[o][:], in_=x_words[o].rearrange("p t r -> p (t r)").bitcast(I32))
 
         def load_w1(e):
-            load_words(w1_word[e], w1_words, (e, e + 1))
+            run = run_of(W1_WORD_RUNS, e)
+            load_words(w1_word[run], w1_words, run)
 
         def slots_of(run):
             return offsets[:, run[0] * C // 16 : run[1] * C // 16]
@@ -109,14 +113,16 @@ def tile_moe_pkd_mlp_relu_kernel(tc, x_words, x_scales, w1_words, w1_scales, w2_
         load_w1(3)
         load_scales(w2_byte[0, 4], w2_scales, (0, 4))
         load_words(w2_word[0, 2], w2_words, (0, 2))
-        load_scales(w1_byte[4, 8], w1_scales, (4, 8))
         load_w1(4)
         load_w1(5)
+        load_scales(w1_byte[4, 6], w1_scales, (4, 6))
         load_words(w2_word[2, 4], w2_words, (2, 4))
         load_w1(6)
+        load_scales(w1_byte[6, 8], w1_scales, (6, 8))
         load_w1(7)
         load_scales(w2_byte[4, 8], w2_scales, (4, 8))
-        load_words(w2_word[4, 8], w2_words, (4, 8))
+        load_words(w2_word[4, 6], w2_words, (4, 6))
+        load_words(w2_word[6, 8], w2_words, (6, 8))
         slot_scale = [slot_byte[:], moved_byte[:].bitcast(U8)]
 
         slot_word = {}
@@ -135,22 +141,22 @@ def tile_moe_pkd_mlp_relu_kernel(tc, x_words, x_scales, w1_words, w1_scales, w2_
                 nc.tensor.transpose(y_bank[half][:, c * P : (c + 1) * P], column, ident[:])
             nc.scalar.copy(out=gate_sb[:, :, 4 * half : 4 * half + 4], in_=y_bank[half][:].rearrange("p (c j) -> p j c", c=4))
 
-        by_slot = {e: held([P, 2, P, 2], BF16, "by_slot%d" % e) for e in range(E) if e != 2}
+        by_slot = {e: held([P, 2, P, 2], BF16, "by_slot%d" % e, "by_slot%d" % e) for e in range(E) if e != 2}
         by_slot[2] = by_slot[1]
-        h_bf = [held([P, 2, C, 4], BF16, "h_bf%d" % c) for c in range(E // 2)]
-        h_word = [held([P, 2 * C], U32, "h_word%d" % c) for c in range(E // 2)]
+        h_bf = [held([P, 2 * C * 4], BF16, "h_bf%d" % c)[:].rearrange("p (m j t) -> p m j t", m=2, t=4) for c in range(E // 2)]
+        h_word = [held([P, 2 * C], U32, "h_word%d" % c, "h_word%d" % c) for c in range(E // 2)]
         h_byte = [held([P, 2 * C], U8, "h_byte%d" % c) for c in range(E // 2)]
 
         def as_words(e):
             return by_slot[e][:].rearrange("j u p d -> j (u p d)").bitcast(F32)
 
         def first_pass(slots, e, o, acc, start, stop):
-            words, scales = run_of(WORD_RUNS[o], slots), run_of(W1_BYTE_RUNS, e)
+            words, weights, scales = run_of(WORD_RUNS[o], slots), run_of(W1_WORD_RUNS, e), run_of(W1_BYTE_RUNS, e)
             nc.tensor.matmul_mx(
                 out=acc[:],
                 lhsT=slot_word[o, words][:, (slots - words[0]) * C : (slots - words[0] + 1) * C].bitcast(FP8X4),
                 lhsT_scale=slot_scale[o][:, slots * C : (slots + 1) * C],
-                rhs=w1_word[e][:, o, :].bitcast(FP4X4),
+                rhs=w1_word[weights][:, PASSES * (e - weights[0]) + o, :].bitcast(FP4X4),
                 rhs_scale=w1_byte[scales][:, PASSES * (e - scales[0]) + o, :].bitcast(U8),
                 start=start,
                 stop=stop,
@@ -191,7 +197,7 @@ def tile_moe_pkd_mlp_relu_kernel(tc, x_words, x_scales, w1_words, w1_scales, w2_
                     stop=True,
                 )
 
-        y_sb = {((2 * c, 2 * c + 2), 1): as_words(2 * c + 3) for c in range(2)}
+        y_sb = {((0, 2), 1): as_words(3), ((2, 4), 0): as_words(5), ((2, 4), 1): None, ((4, 6), 0): None}
         for v in range(2):
             for run in SCATTER_RUNS[v]:
                 if (run, v) not in y_sb:
@@ -208,6 +214,13 @@ def tile_moe_pkd_mlp_relu_kernel(tc, x_words, x_scales, w1_words, w1_scales, w2_
         def scatter(run, v):
             gate_cols = gate_sb[:].rearrange("p j c -> p (j c)")[:, run[0] * C : run[1] * C]
             nc.vector.tensor_tensor(out=window[v][:].indirect(slots_of(run)), in0=y_sb[run, v], in1=gate_cols, op=MULT)
+
+        def gated(c, sums):
+            gate_cols = gate_sb[:].rearrange("p j c -> p (j c)")[:, 2 * c * C : (2 * c + 2) * C]
+            nc.vector.tensor_tensor(out=y_of(c, 1), in0=sums, in1=gate_cols, op=MULT)
+
+        def scatter_on_scalar(c):
+            nc.scalar.activation(out=window[1][:].indirect(slots_of((2 * c, 2 * c + 2))), in_=y_of(c, 1), func=COPY)
 
         def low(bank):
             return bank[:, 0 : BANK // 2]
@@ -241,27 +254,35 @@ def tile_moe_pkd_mlp_relu_kernel(tc, x_words, x_scales, w1_words, w1_scales, w2_
 
         first_layer(4)
         first_layer(5)
-        second_layer(1, 0, low(y_bank[1]))
-        scatter((2, 4), 0)
+        second_products(1, 0, low(y_bank[1]))
         regroup(4, low(turn_bank[1]))
         regroup(5, low(turn_bank[0]))
         second_products(1, 1, high(y_bank[1]))
         quantise(2)
-        nc.scalar.copy(out=y_of(1, 1), in_=high(y_bank[1]))
-        scatter((2, 4), 1)
+        nc.scalar.copy(out=y_of(1, 0), in_=low(y_bank[1]))
+        scatter((2, 4), 0)
 
         first_layer(6)
         first_layer(7)
         regroup(6, low(turn_bank[1]))
-        regroup(7, low(turn_bank[0]))
-        quantise(3)
-        second_layer(2, 0, low(acc_bank[ACC[7]]))
+        quantise(3, 0, 1)
+        second_products(2, 0, low(acc_bank[0]))
+        second_products(2, 1, low(acc_bank[1]))
+        gated(2, low(acc_bank[1]))
+        regroup(7, high(acc_bank[0]))
+        late = held([P, 2, 2 * C], F32, "late", "by_slot7")
+        y_sb[(2, 4), 1], y_sb[(4, 6), 0] = late[:, 0], late[:, 1]
+        gated(1, high(y_bank[1]))
+        nc.scalar.copy(out=y_of(2, 0), in_=low(acc_bank[0]))
+        quantise(3, 1, 2)
         scatter((4, 6), 0)
+        scatter_on_scalar(1)
         second_layer(3, 0, low(y_bank[0]))
+        second_products(3, 1, low(acc_bank[2]))
+        gated(3, low(acc_bank[2]))
         scatter((6, 8), 0)
         nc.sync.dma_start(out=out[0:P, :], in_=window[0][:])
-        second_layer(2, 1, high(acc_bank[ACC[7]]))
-        second_layer(3, 1, low(acc_bank[0]))
-        scatter((4, 8), 1)
+        scatter_on_scalar(2)
+        scatter_on_scalar(3)
         nc.sync.dma_start(out=out[P : 2 * P, 0 : T // 2], in_=window[1][:, 0 : T // 2])
         nc.scalar.dma_start(out=out[P : 2 * P, T // 2 : T], in_=window[1][:, T // 2 : T])

@@ -32,7 +32,7 @@ W2_WORD_RUNS = [(0, 2), (2, 4), (4, 6), (6, 8)]
 W1_WORD_RUNS = [(0, 1), (1, 2), (2, 3), (3, 4), (4, 5), (5, 6), (6, 7), (7, 8)]
 SCATTER_RUNS = [[(0, 2), (2, 4), (4, 6), (6, 8)], [(0, 2), (2, 4), (4, 6), (6, 8)]]
 ACC = [0, 1, 0, 1, 2, 3, 3, 2]
-WARM_SLOTS = [0, 2, 2]
+WARM_SLOTS = [0, 0]
 
 
 def run_of(runs, e):
@@ -241,7 +241,9 @@ def tile_moe_pkd_mlp_relu_kernel(tc, x_words, x_scales, w1_words, w1_scales, w2_
             quantise(0, e, e + 1)
 
         first_layer(2)
-        first_layer(3)
+        first_products(3)
+        for u in range(2):
+            relu(3, slice(u, u + 1))
         second_products(0, 0, low(y_bank[0]))
         nc.vector.tensor_copy(out=y_of(0, 0), in_=low(y_bank[0]))
         scatter((0, 2), 0)
@@ -253,7 +255,9 @@ def tile_moe_pkd_mlp_relu_kernel(tc, x_words, x_scales, w1_words, w1_scales, w2_
         scatter((0, 2), 1)
 
         first_layer(4)
-        first_layer(5)
+        first_products(5)
+        for u in range(2):
+            relu(5, slice(u, u + 1))
         second_products(1, 0, low(y_bank[1]))
         regroup(4, low(turn_bank[1]))
         regroup(5, low(turn_bank[0]))
@@ -263,7 +267,9 @@ def tile_moe_pkd_mlp_relu_kernel(tc, x_words, x_scales, w1_words, w1_scales, w2_
         scatter((2, 4), 0)
 
         first_layer(6)
-        first_layer(7)
+        first_products(7)
+        for u in range(2):
+            relu(7, slice(u, u + 1))
         regroup(6, low(turn_bank[1]))
         quantise(3, 0, 1)
         second_products(2, 0, low(acc_bank[0]))

@@ -114,8 +114,8 @@ def tile_moe_pkd_mlp_relu_kernel(tc, x_words, x_scales, w1_words, w1_scales, w2_
         load_scales(w2_byte[0, 4], w2_scales, (0, 4))
         load_words(w2_word[0, 2], w2_words, (0, 2))
         load_w1(4)
-        load_w1(5)
         load_scales(w1_byte[4, 6], w1_scales, (4, 6))
+        load_w1(5)
         load_words(w2_word[2, 4], w2_words, (2, 4))
         load_w1(6)
         load_scales(w1_byte[6, 8], w1_scales, (6, 8))

@@ -25,7 +25,8 @@ CLEAR = 512
 SHIFT = 16
 GATE_COLS = E * C // P
 
-WORD_RUNS = [[(0, 2), (2, 8)], [(0, 2), (2, 4), (4, 8)]]
+WORD_RUNS = [[(0, 2), (2, 8)], [(0, 1), (1, 2), (2, 4), (4, 8)]]
+BYTE_RUNS = [(0, 4), (4, 8)]
 W1_BYTE_RUNS = [(0, 2), (2, 4), (4, 6), (6, 8)]
 W2_BYTE_RUNS = [(0, 4), (4, 8)]
 W2_WORD_RUNS = [(0, 2), (2, 4), (4, 6), (6, 8)]
@@ -51,12 +52,13 @@ def tile_moe_pkd_mlp_relu_kernel(tc, x_words, x_scales, w1_words, w1_scales, w2_
         offsets = keep.tile([P, E * C // 16], U16, name="offsets")
         x_word = [held([P, T], I32, "x_word%d" % o) for o in range(PASSES)]
         x_byte = held([P, T // 4], I32, "x_byte")
-        w1_word = {run: held([P, PASSES * (run[1] - run[0]), H // 2], I32, "w1_word%d" % run[0]) for run in W1_WORD_RUNS}
+        w1_word = {run: held([P, PASSES * (run[1] - run[0]), H // 2], I32, "w1_word%d" % run[0]) for run in W1_WORD_RUNS[:-1]}
+        last_word = [held([P, H // 2], I32, "last_word%d" % o) for o in range(PASSES)]
         w1_byte = {run: held([P, PASSES * (run[1] - run[0]), H // 4], I32, "w1_byte%d" % run[0]) for run in W1_BYTE_RUNS}
         w2_word = {run: held([P, run[1] - run[0], N // 2], I32, "w2_word%d" % run[0]) for run in W2_WORD_RUNS}
         w2_byte = {run: held([P, run[1] - run[0], N // 4], I32, "w2_byte%d" % run[0]) for run in W2_BYTE_RUNS}
-        slot_byte = held([P, E * C], U8, "slot_byte")
-        moved_byte = held([P, E * C // 4], I32, "moved_byte")
+        slot_byte = {run: held([P, (run[1] - run[0]) * C], U8, "slot_byte%d" % run[0]) for run in BYTE_RUNS}
+        moved_byte = {run: held([P, (run[1] - run[0]) * C // 4], I32, "moved_byte%d" % run[0]) for run in BYTE_RUNS}
         gate_col = held([P, GATE_COLS], F32, "gate_col")
         gate_sb = held([P, P, GATE_COLS], F32, "gate_sb")
         window = [held([P, T], F32, "window%d" % v) for v in range(2)]
@@ -70,7 +72,8 @@ def tile_moe_pkd_mlp_relu_kernel(tc, x_words, x_scales, w1_words, w1_scales, w2_
         nc.vector.memset(ident[:], 0.0)
         nc.vector.memset(zero[:], 0.0)
         nc.vector.memset(w1_byte[0, 2][:], 0)
-        nc.vector.memset(moved_byte[:], 0)
+        nc.vector.memset(moved_byte[0, 4][:], 0)
+        nc.vector.memset(moved_byte[4, 8][:], 0)
         nc.vector.memset(w1_byte[2, 4][:], 0)
         nc.vector.memset(w2_byte[0, 4][:], 0)
         nc.vector.memset(w1_byte[4, 6][:], 0)
@@ -93,6 +96,14 @@ def tile_moe_pkd_mlp_relu_kernel(tc, x_words, x_scales, w1_words, w1_scales, w2_
             run = run_of(W1_WORD_RUNS, e)
             load_words(w1_word[run], w1_words, run)
 
+        def move_scales(run):
+            nc.sync.dma_start(out=moved_byte[run][0 : P - SHIFT, :], in_=slot_byte[run][SHIFT:P, :].bitcast(I32))
+
+        def slot_scale(o, e):
+            run = run_of(BYTE_RUNS, e)
+            plane = slot_byte[run][:] if o == 0 else moved_byte[run][:].bitcast(U8)
+            return plane[:, (e - run[0]) * C : (e - run[0] + 1) * C]
+
         def slots_of(run):
             return offsets[:, run[0] * C // 16 : run[1] * C // 16]
 
@@ -103,27 +114,29 @@ def tile_moe_pkd_mlp_relu_kernel(tc, x_words, x_scales, w1_words, w1_scales, w2_
             nc.sync.dma_start(out=x_byte[r:P:SHIFT, :], in_=token_rows[r].bitcast(I32))
         nc.sync.dma_start(out=gate_col[:], in_=gate[0].rearrange("(j c) -> j c", c=GATE_COLS))
         load_tokens(0)
-        nc.vector.tensor_copy(out=slot_byte[:], in_=x_byte[:].bitcast(U8).indirect(offsets[:]))
+        for run in BYTE_RUNS:
+            nc.vector.tensor_copy(out=slot_byte[run][:], in_=x_byte[:].bitcast(U8).indirect(slots_of(run)))
         load_scales(w1_byte[0, 2], w1_scales, (0, 2))
         load_tokens(1)
-        nc.sync.dma_start(out=moved_byte[0 : P - SHIFT, :], in_=slot_byte[SHIFT:P, :].bitcast(I32))
+        move_scales((0, 4))
         load_w1(1)
         load_scales(w1_byte[2, 4], w1_scales, (2, 4))
         load_w1(2)
         load_w1(3)
         load_scales(w2_byte[0, 4], w2_scales, (0, 4))
         load_words(w2_word[0, 2], w2_words, (0, 2))
+        move_scales((4, 8))
         load_w1(4)
         load_scales(w1_byte[4, 6], w1_scales, (4, 6))
         load_w1(5)
         load_words(w2_word[2, 4], w2_words, (2, 4))
         load_w1(6)
         load_scales(w1_byte[6, 8], w1_scales, (6, 8))
-        load_w1(7)
+        for o in range(PASSES):
+            nc.sync.dma_start(out=last_word[o][:], in_=w1_words[E - 1, o].bitcast(I32))
         load_scales(w2_byte[4, 8], w2_scales, (4, 8))
         load_words(w2_word[4, 6], w2_words, (4, 6))
         load_words(w2_word[6, 8], w2_words, (6, 8))
-        slot_scale = [slot_byte[:], moved_byte[:].bitcast(U8)]
 
         slot_word = {}
         for o in range(PASSES):
@@ -155,8 +168,8 @@ def tile_moe_pkd_mlp_relu_kernel(tc, x_words, x_scales, w1_words, w1_scales, w2_
             nc.tensor.matmul_mx(
                 out=acc[:],
                 lhsT=slot_word[o, words][:, (slots - words[0]) * C : (slots - words[0] + 1) * C].bitcast(FP8X4),
-                lhsT_scale=slot_scale[o][:, slots * C : (slots + 1) * C],
-                rhs=w1_word[weights][:, PASSES * (e - weights[0]) + o, :].bitcast(FP4X4),
+                lhsT_scale=slot_scale(o, slots),
+                rhs=(last_word[o][:] if e == E - 1 else w1_word[weights][:, PASSES * (e - weights[0]) + o, :]).bitcast(FP4X4),
                 rhs_scale=w1_byte[scales][:, PASSES * (e - scales[0]) + o, :].bitcast(U8),
                 start=start,
                 stop=stop,
@@ -197,7 +210,7 @@ def tile_moe_pkd_mlp_relu_kernel(tc, x_words, x_scales, w1_words, w1_scales, w2_
                     stop=True,
                 )
 
-        y_sb = {((0, 2), 1): as_words(3), ((2, 4), 0): as_words(5), ((2, 4), 1): None, ((4, 6), 0): None}
+        y_sb = {((0, 2), 1): as_words(3), ((2, 4), 0): as_words(5)}
         for v in range(2):
             for run in SCATTER_RUNS[v]:
                 if (run, v) not in y_sb:
@@ -261,7 +274,8 @@ def tile_moe_pkd_mlp_relu_kernel(tc, x_words, x_scales, w1_words, w1_scales, w2_
         second_products(1, 0, low(y_bank[1]))
         regroup(4, low(turn_bank[1]))
         regroup(5, low(turn_bank[0]))
-        second_products(1, 1, high(y_bank[1]))
+        second_products(1, 1, high(y_bank[0]))
+        gated(1, high(y_bank[0]))
         quantise(2)
         nc.scalar.copy(out=y_of(1, 0), in_=low(y_bank[1]))
         scatter((2, 4), 0)
@@ -276,19 +290,16 @@ def tile_moe_pkd_mlp_relu_kernel(tc, x_words, x_scales, w1_words, w1_scales, w2_
         second_products(2, 1, low(acc_bank[1]))
         gated(2, low(acc_bank[1]))
         regroup(7, high(acc_bank[0]))
-        late = held([P, 2, 2 * C], F32, "late", "by_slot7")
-        y_sb[(2, 4), 1], y_sb[(4, 6), 0] = late[:, 0], late[:, 1]
-        gated(1, high(y_bank[1]))
         nc.scalar.copy(out=y_of(2, 0), in_=low(acc_bank[0]))
         quantise(3, 1, 2)
         scatter((4, 6), 0)
-        scatter_on_scalar(1)
+        scatter_on_scalar(2)
         second_layer(3, 0, low(y_bank[0]))
         second_products(3, 1, low(acc_bank[2]))
         gated(3, low(acc_bank[2]))
         scatter((6, 8), 0)
         nc.sync.dma_start(out=out[0:P, :], in_=window[0][:])
-        scatter_on_scalar(2)
+        scatter_on_scalar(1)
         scatter_on_scalar(3)
         nc.sync.dma_start(out=out[P : 2 * P, 0 : T // 2], in_=window[1][:, 0 : T // 2])
         nc.scalar.dma_start(out=out[P : 2 * P, T // 2 : T], in_=window[1][:, T // 2 : T])

@@ -20,20 +20,18 @@ MULT = mybir.AluOpType.mult
 
 P = 128
 PASSES = K // 512
+PAIRS = E // 2
 BANK = 512
 CLEAR = 512
 SHIFT = 16
 GATE_COLS = E * C // P
+WARM_UPS = 2
 
 WORD_RUNS = [[(0, 2), (2, 8)], [(0, 1), (1, 2), (2, 4), (4, 8)]]
 BYTE_RUNS = [(0, 4), (4, 8)]
-W1_BYTE_RUNS = [(0, 2), (2, 4), (4, 6), (6, 8)]
 W2_BYTE_RUNS = [(0, 4), (4, 8)]
-W2_WORD_RUNS = [(0, 2), (2, 4), (4, 6), (6, 8)]
-W1_WORD_RUNS = [(0, 1), (1, 2), (2, 3), (3, 4), (4, 5), (5, 6), (6, 7), (7, 8)]
-SCATTER_RUNS = [[(0, 2), (2, 4), (4, 6), (6, 8)], [(0, 2), (2, 4), (4, 6), (6, 8)]]
+BY_PASS = (7,)
 ACC = [0, 1, 0, 1, 2, 3, 3, 2]
-WARM_SLOTS = [0, 0]
 
 
 def run_of(runs, e):
@@ -46,23 +44,23 @@ def tile_moe_pkd_mlp_relu_kernel(tc, x_words, x_scales, w1_words, w1_scales, w2_
         keep = ctx.enter_context(tc.tile_pool(name="keep", bufs=1))
         psum = ctx.enter_context(tc.psum_pool(name="psum", bufs=1))
 
-        def held(shape, dtype, name, tag=""):
-            return keep.tile(shape, dtype, name=name, tag=tag, align_bytes=64)
+        def held(shape, dtype, name):
+            return keep.tile(shape, dtype, name=name, align_bytes=64)
 
         offsets = keep.tile([P, E * C // 16], U16, name="offsets")
         x_word = [held([P, T], I32, "x_word%d" % o) for o in range(PASSES)]
         x_byte = held([P, T // 4], I32, "x_byte")
-        w1_word = {run: held([P, PASSES * (run[1] - run[0]), H // 2], I32, "w1_word%d" % run[0]) for run in W1_WORD_RUNS[:-1]}
-        last_word = [held([P, H // 2], I32, "last_word%d" % o) for o in range(PASSES)]
-        w1_byte = {run: held([P, PASSES * (run[1] - run[0]), H // 4], I32, "w1_byte%d" % run[0]) for run in W1_BYTE_RUNS}
-        w2_word = {run: held([P, run[1] - run[0], N // 2], I32, "w2_word%d" % run[0]) for run in W2_WORD_RUNS}
+        w1_word = {e: held([P, PASSES, H // 2], I32, "w1_word%d" % e) for e in range(E) if e not in BY_PASS}
+        w1_pass = {(e, o): held([P, H // 2], I32, "w1_pass%d_%d" % (e, o)) for e in BY_PASS for o in range(PASSES)}
+        w1_byte = [held([P, 2 * PASSES, H // 4], I32, "w1_byte%d" % c) for c in range(PAIRS)]
+        w2_word = [held([P, 2, N // 2], I32, "w2_word%d" % c) for c in range(PAIRS)]
         w2_byte = {run: held([P, run[1] - run[0], N // 4], I32, "w2_byte%d" % run[0]) for run in W2_BYTE_RUNS}
         slot_byte = {run: held([P, (run[1] - run[0]) * C], U8, "slot_byte%d" % run[0]) for run in BYTE_RUNS}
         moved_byte = {run: held([P, (run[1] - run[0]) * C // 4], I32, "moved_byte%d" % run[0]) for run in BYTE_RUNS}
         gate_col = held([P, GATE_COLS], F32, "gate_col")
         gate_sb = held([P, P, GATE_COLS], F32, "gate_sb")
         window = [held([P, T], F32, "window%d" % v) for v in range(2)]
-        zero = held([P, 8], F32, "zero")
+        zero = held([P, 1], F32, "zero")
         ident = held([P, P], F32, "ident")
         acc_bank = [psum.tile([P, BANK], F32, name="acc_bank%d" % b) for b in range(4)]
         y_bank = [psum.tile([P, BANK], F32, name="y_bank%d" % b) for b in range(2)]
@@ -71,21 +69,15 @@ def tile_moe_pkd_mlp_relu_kernel(tc, x_words, x_scales, w1_words, w1_scales, w2_
         nc.gpsimd.memset(x_byte[:], 0)
         nc.vector.memset(ident[:], 0.0)
         nc.vector.memset(zero[:], 0.0)
-        nc.vector.memset(w1_byte[0, 2][:], 0)
-        nc.vector.memset(moved_byte[0, 4][:], 0)
-        nc.vector.memset(moved_byte[4, 8][:], 0)
-        nc.vector.memset(w1_byte[2, 4][:], 0)
-        nc.vector.memset(w2_byte[0, 4][:], 0)
-        nc.vector.memset(w1_byte[4, 6][:], 0)
-        nc.vector.memset(w1_byte[6, 8][:], 0)
-        nc.vector.memset(w2_byte[4, 8][:], 0)
+        for plane in (w1_byte[0], moved_byte[0, 4], moved_byte[4, 8], w1_byte[1], w2_byte[0, 4], w1_byte[2], w1_byte[3], w2_byte[4, 8]):
+            nc.vector.memset(plane[:], 0)
         make_identity(nc, ident[:], nomemset=True)
 
-        def load_words(tile, words, run):
-            nc.sync.dma_start(out=tile[:], in_=words[run[0] : run[1]].rearrange("e s p b -> p (e s) b").bitcast(I32))
+        def load_words(tile, words, a, b):
+            nc.sync.dma_start(out=tile[:], in_=words[a:b].rearrange("e s p b -> p (e s) b").bitcast(I32))
 
-        def load_scales(plane, scales, run):
-            rows = scales[run[0] : run[1]].rearrange("e s (q r) i -> r q (e s) i", r=4)
+        def load_scales(plane, scales, a, b):
+            rows = scales[a:b].rearrange("e s (q r) i -> r q (e s) i", r=4)
             for r in range(4):
                 nc.sync.dma_start(out=plane[r:P:32], in_=rows[r].bitcast(I32))
 
@@ -93,19 +85,23 @@ def tile_moe_pkd_mlp_relu_kernel(tc, x_words, x_scales, w1_words, w1_scales, w2_
             nc.sync.dma_start(out=x_word[o][:], in_=x_words[o].rearrange("p t r -> p (t r)").bitcast(I32))
 
         def load_w1(e):
-            run = run_of(W1_WORD_RUNS, e)
-            load_words(w1_word[run], w1_words, run)
+            if e in BY_PASS:
+                for o in range(PASSES):
+                    nc.sync.dma_start(out=w1_pass[e, o][:], in_=w1_words[e, o].bitcast(I32))
+            else:
+                load_words(w1_word[e], w1_words, e, e + 1)
+
+        def load_w1_scales(c):
+            load_scales(w1_byte[c], w1_scales, 2 * c, 2 * c + 2)
+
+        def load_w2(c):
+            load_words(w2_word[c], w2_words, 2 * c, 2 * c + 2)
 
         def move_scales(run):
             nc.sync.dma_start(out=moved_byte[run][0 : P - SHIFT, :], in_=slot_byte[run][SHIFT:P, :].bitcast(I32))
 
-        def slot_scale(o, e):
-            run = run_of(BYTE_RUNS, e)
-            plane = slot_byte[run][:] if o == 0 else moved_byte[run][:].bitcast(U8)
-            return plane[:, (e - run[0]) * C : (e - run[0] + 1) * C]
-
-        def slots_of(run):
-            return offsets[:, run[0] * C // 16 : run[1] * C // 16]
+        def slots_of(a, b):
+            return offsets[:, a * C // 16 : b * C // 16]
 
         nc.sync.dma_start(offsets[:], offs)
         load_w1(0)
@@ -115,77 +111,79 @@ def tile_moe_pkd_mlp_relu_kernel(tc, x_words, x_scales, w1_words, w1_scales, w2_
         nc.sync.dma_start(out=gate_col[:], in_=gate[0].rearrange("(j c) -> j c", c=GATE_COLS))
         load_tokens(0)
         for run in BYTE_RUNS:
-            nc.vector.tensor_copy(out=slot_byte[run][:], in_=x_byte[:].bitcast(U8).indirect(slots_of(run)))
-        load_scales(w1_byte[0, 2], w1_scales, (0, 2))
+            nc.vector.tensor_copy(out=slot_byte[run][:], in_=x_byte[:].bitcast(U8).indirect(slots_of(*run)))
+        load_w1_scales(0)
         load_tokens(1)
-        move_scales((0, 4))
+        move_scales(BYTE_RUNS[0])
         load_w1(1)
-        load_scales(w1_byte[2, 4], w1_scales, (2, 4))
+        load_w1_scales(1)
         load_w1(2)
         load_w1(3)
-        load_scales(w2_byte[0, 4], w2_scales, (0, 4))
-        load_words(w2_word[0, 2], w2_words, (0, 2))
-        move_scales((4, 8))
+        load_scales(w2_byte[0, 4], w2_scales, 0, 4)
+        load_w2(0)
         load_w1(4)
-        load_scales(w1_byte[4, 6], w1_scales, (4, 6))
+        move_scales(BYTE_RUNS[1])
+        load_w1_scales(2)
         load_w1(5)
-        load_words(w2_word[2, 4], w2_words, (2, 4))
+        load_w2(1)
         load_w1(6)
-        load_scales(w1_byte[6, 8], w1_scales, (6, 8))
-        for o in range(PASSES):
-            nc.sync.dma_start(out=last_word[o][:], in_=w1_words[E - 1, o].bitcast(I32))
-        load_scales(w2_byte[4, 8], w2_scales, (4, 8))
-        load_words(w2_word[4, 6], w2_words, (4, 6))
-        load_words(w2_word[6, 8], w2_words, (6, 8))
+        load_w1_scales(3)
+        load_w1(7)
+        load_scales(w2_byte[4, 8], w2_scales, 4, 8)
+        load_w2(2)
+        load_w2(3)
 
         slot_word = {}
         for o in range(PASSES):
             for run in WORD_RUNS[o]:
                 slot_word[o, run] = held([P, (run[1] - run[0]) * C], U32, "slot_word%d_%d" % (o, run[0]))
-                nc.vector.tensor_copy(out=slot_word[o, run][:], in_=x_word[o][:].bitcast(U32).indirect(slots_of(run)))
+                nc.vector.tensor_copy(out=slot_word[o, run][:], in_=x_word[o][:].bitcast(U32).indirect(slots_of(*run)))
 
         for v in range(2):
             for a in range(0, T, CLEAR):
                 nc.scalar.activation(out=window[v][:, a : a + CLEAR], in_=zero[:, 0:1].to_broadcast([P, CLEAR]), func=RELU)
 
-        for half in range(2):
-            for c in range(4):
-                column = gate_col[:, 4 * half + c : 4 * half + c + 1].to_broadcast([P, P])
-                nc.tensor.transpose(y_bank[half][:, c * P : (c + 1) * P], column, ident[:])
-            nc.scalar.copy(out=gate_sb[:, :, 4 * half : 4 * half + 4], in_=y_bank[half][:].rearrange("p (c j) -> p j c", c=4))
+        for b in range(2):
+            for g in range(4):
+                column = gate_col[:, 4 * b + g : 4 * b + g + 1].to_broadcast([P, P])
+                nc.tensor.transpose(y_bank[b][:, g * P : (g + 1) * P], column, ident[:])
+            nc.scalar.copy(out=gate_sb[:, :, 4 * b : 4 * b + 4], in_=y_bank[b][:].rearrange("p (g j) -> p j g", g=4))
 
-        by_slot = {e: held([P, 2, P, 2], BF16, "by_slot%d" % e, "by_slot%d" % e) for e in range(E) if e != 2}
+        by_slot = {e: held([P, 2, P, 2], BF16, "by_slot%d" % e) for e in range(E) if e != 2}
         by_slot[2] = by_slot[1]
-        h_bf = [held([P, 2 * C * 4], BF16, "h_bf%d" % c)[:].rearrange("p (m j t) -> p m j t", m=2, t=4) for c in range(E // 2)]
-        h_word = [held([P, 2 * C], U32, "h_word%d" % c, "h_word%d" % c) for c in range(E // 2)]
-        h_byte = [held([P, 2 * C], U8, "h_byte%d" % c) for c in range(E // 2)]
+        h_bf = [held([P, 2 * C * 4], BF16, "h_bf%d" % c)[:].rearrange("p (m j t) -> p m j t", m=2, t=4) for c in range(PAIRS)]
+        h_word = [held([P, 2 * C], U32, "h_word%d" % c) for c in range(PAIRS)]
+        h_byte = [held([P, 2 * C], U8, "h_byte%d" % c) for c in range(PAIRS)]
 
         def as_words(e):
             return by_slot[e][:].rearrange("j u p d -> j (u p d)").bitcast(F32)
 
-        def first_pass(slots, e, o, acc, start, stop):
-            words, weights, scales = run_of(WORD_RUNS[o], slots), run_of(W1_WORD_RUNS, e), run_of(W1_BYTE_RUNS, e)
+        def first_pass(e, o, acc, start, stop):
+            words, rows = run_of(WORD_RUNS[o], e), run_of(BYTE_RUNS, e)
+            plane = slot_byte[rows][:] if o == 0 else moved_byte[rows][:].bitcast(U8)
+            weights = w1_pass[e, o][:] if e in BY_PASS else w1_word[e][:, o, :]
             nc.tensor.matmul_mx(
                 out=acc[:],
-                lhsT=slot_word[o, words][:, (slots - words[0]) * C : (slots - words[0] + 1) * C].bitcast(FP8X4),
-                lhsT_scale=slot_scale(o, slots),
-                rhs=(last_word[o][:] if e == E - 1 else w1_word[weights][:, PASSES * (e - weights[0]) + o, :]).bitcast(FP4X4),
-                rhs_scale=w1_byte[scales][:, PASSES * (e - scales[0]) + o, :].bitcast(U8),
+                lhsT=slot_word[o, words][:, (e - words[0]) * C : (e - words[0] + 1) * C].bitcast(FP8X4),
+                lhsT_scale=plane[:, (e - rows[0]) * C : (e - rows[0] + 1) * C],
+                rhs=weights.bitcast(FP4X4),
+                rhs_scale=w1_byte[e // 2][:, PASSES * (e % 2) + o, :].bitcast(U8),
                 start=start,
                 stop=stop,
             )
 
-        def relu(e, halves=slice(0, 2)):
+        def relu(e, words=slice(0, 2)):
             sums = acc_bank[ACC[e]][:].rearrange("j (p u d) -> j u p d", u=2, d=2)
-            nc.scalar.activation(out=by_slot[e][:, halves], in_=sums[:, halves], func=RELU)
-
-        def first_products(e):
-            for o in range(PASSES):
-                first_pass(e, e, o, acc_bank[ACC[e]], o == 0, o == PASSES - 1)
+            nc.scalar.activation(out=by_slot[e][:, words], in_=sums[:, words], func=RELU)
 
         def first_layer(e):
-            first_products(e)
-            relu(e)
+            for o in range(PASSES):
+                first_pass(e, o, acc_bank[ACC[e]], o == 0, o == PASSES - 1)
+            if e % 2 == 0:
+                relu(e)
+            else:
+                for u in range(2):
+                    relu(e, slice(u, u + 1))
 
         def regroup(e, turned):
             for u in range(2):
@@ -199,41 +197,34 @@ def tile_moe_pkd_mlp_relu_kernel(tc, x_words, x_scales, w1_words, w1_scales, w2_
         def second_products(c, v, sums):
             for m in range(2):
                 e = 2 * c + m
-                words, scales = run_of(W2_WORD_RUNS, e), run_of(W2_BYTE_RUNS, e)
+                rows = run_of(W2_BYTE_RUNS, e)
                 nc.tensor.matmul_mx(
                     out=sums[:, m * C : (m + 1) * C],
-                    lhsT=w2_word[words][:, e - words[0], v * P // 2 : (v + 1) * P // 2].bitcast(FP4X4),
-                    lhsT_scale=w2_byte[scales][:, e - scales[0], v * P // 4 : (v + 1) * P // 4].bitcast(U8),
+                    lhsT=w2_word[c][:, m, v * P // 2 : (v + 1) * P // 2].bitcast(FP4X4),
+                    lhsT_scale=w2_byte[rows][:, e - rows[0], v * P // 4 : (v + 1) * P // 4].bitcast(U8),
                     rhs=h_word[c][:, m * C : (m + 1) * C].bitcast(FP8X4),
                     rhs_scale=h_byte[c][:, m * C : (m + 1) * C],
                     start=True,
                     stop=True,
                 )
 
-        y_sb = {((0, 2), 1): as_words(3), ((2, 4), 0): as_words(5)}
+        y_sb = {(0, 1): as_words(3), (1, 0): as_words(5)}
         for v in range(2):
-            for run in SCATTER_RUNS[v]:
-                if (run, v) not in y_sb:
-                    y_sb[run, v] = held([P, (run[1] - run[0]) * C], F32, "y_sb%d_%d" % (run[0], v))[:]
+            for c in range(PAIRS):
+                if (c, v) not in y_sb:
+                    y_sb[c, v] = held([P, 2 * C], F32, "y_sb%d_%d" % (c, v))[:]
 
-        def y_of(c, v):
-            run = run_of(SCATTER_RUNS[v], 2 * c)
-            return y_sb[run, v][:, (2 * c - run[0]) * C : (2 * c + 2 - run[0]) * C]
+        def gate_of(c):
+            return gate_sb[:].rearrange("p j g -> p (j g)")[:, 2 * c * C : (2 * c + 2) * C]
 
-        def second_layer(c, v, sums):
-            second_products(c, v, sums)
-            nc.scalar.copy(out=y_of(c, v), in_=sums)
+        def scatter_times_gate(c, v):
+            nc.vector.tensor_tensor(out=window[v][:].indirect(slots_of(2 * c, 2 * c + 2)), in0=y_sb[c, v], in1=gate_of(c), op=MULT)
 
-        def scatter(run, v):
-            gate_cols = gate_sb[:].rearrange("p j c -> p (j c)")[:, run[0] * C : run[1] * C]
-            nc.vector.tensor_tensor(out=window[v][:].indirect(slots_of(run)), in0=y_sb[run, v], in1=gate_cols, op=MULT)
+        def lower_times_gate(c, sums):
+            nc.vector.tensor_tensor(out=y_sb[c, 1], in0=sums, in1=gate_of(c), op=MULT)
 
-        def gated(c, sums):
-            gate_cols = gate_sb[:].rearrange("p j c -> p (j c)")[:, 2 * c * C : (2 * c + 2) * C]
-            nc.vector.tensor_tensor(out=y_of(c, 1), in0=sums, in1=gate_cols, op=MULT)
-
-        def scatter_on_scalar(c):
-            nc.scalar.activation(out=window[1][:].indirect(slots_of((2 * c, 2 * c + 2))), in_=y_of(c, 1), func=COPY)
+        def scatter_lower(c):
+            nc.scalar.activation(out=window[1][:].indirect(slots_of(2 * c, 2 * c + 2)), in_=y_sb[c, 1], func=COPY)
 
         def low(bank):
             return bank[:, 0 : BANK // 2]
@@ -241,65 +232,58 @@ def tile_moe_pkd_mlp_relu_kernel(tc, x_words, x_scales, w1_words, w1_scales, w2_
         def high(bank):
             return bank[:, BANK // 2 : BANK]
 
-        first_pass(0, 0, 0, acc_bank[ACC[0]], True, False)
-        for slots in WARM_SLOTS:
-            first_pass(slots, 0, 0, acc_bank[3], True, True)
-        first_pass(0, 0, 1, acc_bank[ACC[0]], False, True)
+        first_pass(0, 0, acc_bank[ACC[0]], True, False)
+        for repeat in range(WARM_UPS):
+            first_pass(0, 0, acc_bank[3], True, True)
+        first_pass(0, 1, acc_bank[ACC[0]], False, True)
         relu(0)
-        first_products(1)
-        for u in range(2):
-            relu(1, slice(u, u + 1))
+        first_layer(1)
         for e in range(2):
             regroup(e, low(turn_bank[e]))
             quantise(0, e, e + 1)
 
         first_layer(2)
-        first_products(3)
-        for u in range(2):
-            relu(3, slice(u, u + 1))
+        first_layer(3)
         second_products(0, 0, low(y_bank[0]))
-        nc.vector.tensor_copy(out=y_of(0, 0), in_=low(y_bank[0]))
-        scatter((0, 2), 0)
+        nc.vector.tensor_copy(out=y_sb[0, 0], in_=low(y_bank[0]))
+        scatter_times_gate(0, 0)
         second_products(0, 1, high(turn_bank[0]))
         regroup(2, low(turn_bank[0]))
         regroup(3, high(y_bank[0]))
         quantise(1)
-        nc.scalar.copy(out=y_of(0, 1), in_=high(turn_bank[0]))
-        scatter((0, 2), 1)
+        nc.scalar.copy(out=y_sb[0, 1], in_=high(turn_bank[0]))
+        scatter_times_gate(0, 1)
 
         first_layer(4)
-        first_products(5)
-        for u in range(2):
-            relu(5, slice(u, u + 1))
+        first_layer(5)
         second_products(1, 0, low(y_bank[1]))
         regroup(4, low(turn_bank[1]))
         regroup(5, low(turn_bank[0]))
         second_products(1, 1, high(y_bank[0]))
-        gated(1, high(y_bank[0]))
+        lower_times_gate(1, high(y_bank[0]))
         quantise(2)
-        nc.scalar.copy(out=y_of(1, 0), in_=low(y_bank[1]))
-        scatter((2, 4), 0)
+        nc.scalar.copy(out=y_sb[1, 0], in_=low(y_bank[1]))
+        scatter_times_gate(1, 0)
 
         first_layer(6)
-        first_products(7)
-        for u in range(2):
-            relu(7, slice(u, u + 1))
+        first_layer(7)
         regroup(6, low(turn_bank[1]))
         quantise(3, 0, 1)
         second_products(2, 0, low(acc_bank[0]))
         second_products(2, 1, low(acc_bank[1]))
-        gated(2, low(acc_bank[1]))
+        lower_times_gate(2, low(acc_bank[1]))
         regroup(7, high(acc_bank[0]))
-        nc.scalar.copy(out=y_of(2, 0), in_=low(acc_bank[0]))
+        nc.scalar.copy(out=y_sb[2, 0], in_=low(acc_bank[0]))
         quantise(3, 1, 2)
-        scatter((4, 6), 0)
-        scatter_on_scalar(2)
-        second_layer(3, 0, low(y_bank[0]))
+        scatter_times_gate(2, 0)
+        scatter_lower(2)
+        second_products(3, 0, low(y_bank[0]))
+        nc.scalar.copy(out=y_sb[3, 0], in_=low(y_bank[0]))
         second_products(3, 1, low(acc_bank[2]))
-        gated(3, low(acc_bank[2]))
-        scatter((6, 8), 0)
+        lower_times_gate(3, low(acc_bank[2]))
+        scatter_times_gate(3, 0)
         nc.sync.dma_start(out=out[0:P, :], in_=window[0][:])
-        scatter_on_scalar(1)
-        scatter_on_scalar(3)
+        scatter_lower(1)
+        scatter_lower(3)
         nc.sync.dma_start(out=out[P : 2 * P, 0 : T // 2], in_=window[1][:, 0 : T // 2])
         nc.scalar.dma_start(out=out[P : 2 * P, T // 2 : T], in_=window[1][:, T // 2 : T])

@@ -30,7 +30,7 @@ WARM_UPS = 2
 WORD_RUNS = [[(0, 2), (2, 8)], [(0, 1), (1, 2), (2, 4), (4, 8)]]
 BYTE_RUNS = [(0, 4), (4, 8)]
 W2_BYTE_RUNS = [(0, 4), (4, 8)]
-BY_PASS = (7,)
+BY_PASS = (5, 7)
 ACC = [0, 1, 0, 1, 2, 3, 3, 2]
 
 
@@ -50,7 +50,8 @@ def tile_moe_pkd_mlp_relu_kernel(tc, x_words, x_scales, w1_words, w1_scales, w2_
         offsets = keep.tile([P, E * C // 16], U16, name="offsets")
         x_word = [held([P, T], I32, "x_word%d" % o) for o in range(PASSES)]
         x_byte = held([P, T // 4], I32, "x_byte")
-        w1_word = {e: held([P, PASSES, H // 2], I32, "w1_word%d" % e) for e in range(E) if e not in BY_PASS}
+        w1_word = {e: held([P, PASSES, H // 2], I32, "w1_word%d" % e) for e in range(E) if e not in BY_PASS + (2, 3)}
+        w1_two = held([P, 2 * PASSES, H // 2], I32, "w1_two")
         w1_pass = {(e, o): held([P, H // 2], I32, "w1_pass%d_%d" % (e, o)) for e in BY_PASS for o in range(PASSES)}
         w1_byte = [held([P, 2 * PASSES, H // 4], I32, "w1_byte%d" % c) for c in range(PAIRS)]
         w2_word = [held([P, 2, N // 2], I32, "w2_word%d" % c) for c in range(PAIRS)]
@@ -117,8 +118,7 @@ def tile_moe_pkd_mlp_relu_kernel(tc, x_words, x_scales, w1_words, w1_scales, w2_
         move_scales(BYTE_RUNS[0])
         load_w1(1)
         load_w1_scales(1)
-        load_w1(2)
-        load_w1(3)
+        load_words(w1_two, w1_words, 2, 4)
         load_scales(w2_byte[0, 4], w2_scales, 0, 4)
         load_w2(0)
         load_w1(4)
@@ -161,7 +161,7 @@ def tile_moe_pkd_mlp_relu_kernel(tc, x_words, x_scales, w1_words, w1_scales, w2_
         def first_pass(e, o, acc, start, stop):
             words, rows = run_of(WORD_RUNS[o], e), run_of(BYTE_RUNS, e)
             plane = slot_byte[rows][:] if o == 0 else moved_byte[rows][:].bitcast(U8)
-            weights = w1_pass[e, o][:] if e in BY_PASS else w1_word[e][:, o, :]
+            weights = w1_pass[e, o][:] if e in BY_PASS else w1_two[:, PASSES * (e - 2) + o, :] if e in (2, 3) else w1_word[e][:, o, :]
             nc.tensor.matmul_mx(
                 out=acc[:],
                 lhsT=slot_word[o, words][:, (e - words[0]) * C : (e - words[0] + 1) * C].bitcast(FP8X4),
@@ -260,8 +260,9 @@ def tile_moe_pkd_mlp_relu_kernel(tc, x_words, x_scales, w1_words, w1_scales, w2_
         regroup(4, low(turn_bank[1]))
         regroup(5, low(turn_bank[0]))
         second_products(1, 1, high(y_bank[0]))
+        quantise(2, 0, 1)
         lower_times_gate(1, high(y_bank[0]))
-        quantise(2)
+        quantise(2, 1, 2)
         nc.scalar.copy(out=y_sb[1, 0], in_=low(y_bank[1]))
         scatter_times_gate(1, 0)
 

@@ -27,7 +27,7 @@ SHIFT = 16
 GATE_COLS = E * C // P
 WARM_UPS = 2
 
-WORD_RUNS = [[(0, 2), (2, 8)], [(0, 1), (1, 2), (2, 4), (4, 8)]]
+WORD_RUNS = [[(0, 2), (2, 8)], [(0, 1), (1, 2), (2, 4), (4, 6), (6, 8)]]
 BYTE_RUNS = [(0, 4), (4, 8)]
 W2_BYTE_RUNS = [(0, 4), (4, 8)]
 BY_PASS = (5, 7)
@@ -44,14 +44,15 @@ def tile_moe_pkd_mlp_relu_kernel(tc, x_words, x_scales, w1_words, w1_scales, w2_
         keep = ctx.enter_context(tc.tile_pool(name="keep", bufs=1))
         psum = ctx.enter_context(tc.psum_pool(name="psum", bufs=1))
 
-        def held(shape, dtype, name):
-            return keep.tile(shape, dtype, name=name, align_bytes=64)
+        def held(shape, dtype, name, tag=None):
+            return keep.tile(shape, dtype, name=name, tag=tag or name, align_bytes=64)
 
         offsets = keep.tile([P, E * C // 16], U16, name="offsets")
         x_word = [held([P, T], I32, "x_word%d" % o) for o in range(PASSES)]
         x_byte = held([P, T // 4], I32, "x_byte")
-        w1_word = {e: held([P, PASSES, H // 2], I32, "w1_word%d" % e) for e in range(E) if e not in BY_PASS + (2, 3)}
-        w1_two = held([P, 2 * PASSES, H // 2], I32, "w1_two")
+        w1_word = {e: held([P, PASSES, H // 2], I32, "w1_word%d" % e) for e in range(E) if e in (2, 3, 4, 6)}
+        w1_head = held([P, 2, H // 2], I32, "w1_head")
+        w1_late = [held([P, H // 2], I32, "w1_late%d" % e) for e in range(2)]
         w1_pass = {(e, o): held([P, H // 2], I32, "w1_pass%d_%d" % (e, o)) for e in BY_PASS for o in range(PASSES)}
         w1_byte = [held([P, 2 * PASSES, H // 4], I32, "w1_byte%d" % c) for c in range(PAIRS)]
         w2_word = [held([P, 2, N // 2], I32, "w2_word%d" % c) for c in range(PAIRS)]
@@ -105,7 +106,7 @@ def tile_moe_pkd_mlp_relu_kernel(tc, x_words, x_scales, w1_words, w1_scales, w2_
             return offsets[:, a * C // 16 : b * C // 16]
 
         nc.sync.dma_start(offsets[:], offs)
-        load_w1(0)
+        nc.sync.dma_start(out=w1_head[:], in_=w1_words[0:2, 0].rearrange("e p b -> p e b").bitcast(I32))
         token_rows = x_scales.rearrange("o (q r) t -> r q o t", r=4)
         for r in range(4):
             nc.sync.dma_start(out=x_byte[r:P:SHIFT, :], in_=token_rows[r].bitcast(I32))
@@ -116,9 +117,11 @@ def tile_moe_pkd_mlp_relu_kernel(tc, x_words, x_scales, w1_words, w1_scales, w2_
         load_w1_scales(0)
         load_tokens(1)
         move_scales(BYTE_RUNS[0])
-        load_w1(1)
+        for e in range(2):
+            nc.sync.dma_start(out=w1_late[e][:], in_=w1_words[e, 1].bitcast(I32))
         load_w1_scales(1)
-        load_words(w1_two, w1_words, 2, 4)
+        load_w1(2)
+        load_w1(3)
         load_scales(w2_byte[0, 4], w2_scales, 0, 4)
         load_w2(0)
         load_w1(4)
@@ -134,10 +137,15 @@ def tile_moe_pkd_mlp_relu_kernel(tc, x_words, x_scales, w1_words, w1_scales, w2_
         load_w2(3)
 
         slot_word = {}
+
+        def gather_words(o, run, tag=None):
+            slot_word[o, run] = held([P, (run[1] - run[0]) * C], U32, "slot_word%d_%d" % (o, run[0]), tag)
+            nc.vector.tensor_copy(out=slot_word[o, run][:], in_=x_word[o][:].bitcast(U32).indirect(slots_of(*run)))
+
         for o in range(PASSES):
             for run in WORD_RUNS[o]:
-                slot_word[o, run] = held([P, (run[1] - run[0]) * C], U32, "slot_word%d_%d" % (o, run[0]))
-                nc.vector.tensor_copy(out=slot_word[o, run][:], in_=x_word[o][:].bitcast(U32).indirect(slots_of(*run)))
+                if o == 0 or run[0] < 4:
+                    gather_words(o, run)
 
         for v in range(2):
             for a in range(0, T, CLEAR):
@@ -161,7 +169,10 @@ def tile_moe_pkd_mlp_relu_kernel(tc, x_words, x_scales, w1_words, w1_scales, w2_
         def first_pass(e, o, acc, start, stop):
             words, rows = run_of(WORD_RUNS[o], e), run_of(BYTE_RUNS, e)
             plane = slot_byte[rows][:] if o == 0 else moved_byte[rows][:].bitcast(U8)
-            weights = w1_pass[e, o][:] if e in BY_PASS else w1_two[:, PASSES * (e - 2) + o, :] if e in (2, 3) else w1_word[e][:, o, :]
+            if e < 2:
+                weights = w1_late[e][:] if o else w1_head[:, e, :]
+            else:
+                weights = w1_pass[e, o][:] if e in BY_PASS else w1_word[e][:, o, :]
             nc.tensor.matmul_mx(
                 out=acc[:],
                 lhsT=slot_word[o, words][:, (e - words[0]) * C : (e - words[0] + 1) * C].bitcast(FP8X4),
@@ -233,14 +244,19 @@ def tile_moe_pkd_mlp_relu_kernel(tc, x_words, x_scales, w1_words, w1_scales, w2_
             return bank[:, BANK // 2 : BANK]
 
         first_pass(0, 0, acc_bank[ACC[0]], True, False)
+        first_pass(1, 0, acc_bank[ACC[1]], True, False)
         for repeat in range(WARM_UPS):
             first_pass(0, 0, acc_bank[3], True, True)
         first_pass(0, 1, acc_bank[ACC[0]], False, True)
         relu(0)
-        first_layer(1)
+        first_pass(1, 1, acc_bank[ACC[1]], False, True)
+        sums = acc_bank[ACC[1]][:].rearrange("j (p u d) -> j u p d", u=2, d=2)
+        nc.vector.tensor_scalar_max(out=by_slot[1][:], in0=sums, scalar1=0.0)
+        gather_words(1, (4, 6), "slot_word1_1")
         for e in range(2):
             regroup(e, low(turn_bank[e]))
             quantise(0, e, e + 1)
+        gather_words(1, (6, 8), "h_bf0")
 
         first_layer(2)
         first_layer(3)

@@ -27,7 +27,7 @@ SHIFT = 16
 GATE_COLS = E * C // P
 WARM_UPS = 2
 
-WORD_RUNS = [[(0, 2), (2, 8)], [(0, 1), (1, 2), (2, 4), (4, 6), (6, 8)]]
+WORD_RUNS = [[(0, 2), (2, 8)], [(0, 1), (1, 2), (2, 5), (5, 7), (7, 8)]]
 BYTE_RUNS = [(0, 4), (4, 8)]
 W2_BYTE_RUNS = [(0, 4), (4, 8)]
 BY_PASS = (5, 7)
@@ -144,7 +144,7 @@ def tile_moe_pkd_mlp_relu_kernel(tc, x_words, x_scales, w1_words, w1_scales, w2_
 
         for o in range(PASSES):
             for run in WORD_RUNS[o]:
-                if o == 0 or run[0] < 4:
+                if o == 0 or run[0] < 5:
                     gather_words(o, run)
 
         for v in range(2):
@@ -252,11 +252,11 @@ def tile_moe_pkd_mlp_relu_kernel(tc, x_words, x_scales, w1_words, w1_scales, w2_
         first_pass(1, 1, acc_bank[ACC[1]], False, True)
         sums = acc_bank[ACC[1]][:].rearrange("j (p u d) -> j u p d", u=2, d=2)
         nc.vector.tensor_scalar_max(out=by_slot[1][:], in0=sums, scalar1=0.0)
-        gather_words(1, (4, 6), "slot_word1_1")
+        gather_words(1, (5, 7), "slot_word1_1")
         for e in range(2):
             regroup(e, low(turn_bank[e]))
             quantise(0, e, e + 1)
-        gather_words(1, (6, 8), "h_bf0")
+        gather_words(1, (7, 8), "h_bf0")
 
         first_layer(2)
         first_layer(3)

from contextlib import ExitStack

import concourse.mybir as mybir
from concourse.masks import make_identity

K, T, E, C, H, N = 1024, 2048, 8, 128, 512, 256
FLOPS = 2 * E * C * (K * H + H * N)

F32 = mybir.dt.float32
BF16 = mybir.dt.bfloat16
I32 = mybir.dt.int32
U32 = mybir.dt.uint32
U16 = mybir.dt.uint16
U8 = mybir.dt.uint8
FP8X4 = mybir.dt.float8_e4m3fn_x4
FP4X4 = mybir.dt.float4_e2m1fn_x4
RELU = mybir.ActivationFunctionType.Relu
COPY = mybir.ActivationFunctionType.Copy
MULT = mybir.AluOpType.mult

P = 128
PASSES = K // 512
PAIRS = E // 2
BANK = 512
CLEAR = 512
SHIFT = 16
GATE_COLS = E * C // P
WARM_UPS = 2

WORD_RUNS = [[(0, 2), (2, 8)], [(0, 1), (1, 2), (2, 5), (5, 7), (7, 8)]]
BYTE_RUNS = [(0, 4), (4, 8)]
W2_BYTE_RUNS = [(0, 4), (4, 8)]
BY_PASS = (5, 7)
ACC = [0, 1, 0, 1, 2, 3, 3, 2]


def run_of(runs, e):
    return [run for run in runs if run[0] <= e < run[1]][0]


def tile_moe_pkd_mlp_relu_kernel(tc, x_words, x_scales, w1_words, w1_scales, w2_words, w2_scales, gate, offs, out):
    nc = tc.nc
    with ExitStack() as ctx:
        keep = ctx.enter_context(tc.tile_pool(name="keep", bufs=1))
        psum = ctx.enter_context(tc.psum_pool(name="psum", bufs=1))

        def held(shape, dtype, name, tag=None):
            return keep.tile(shape, dtype, name=name, tag=tag or name, align_bytes=64)

        offsets = keep.tile([P, E * C // 16], U16, name="offsets")
        x_word = [held([P, T], I32, "x_word%d" % o) for o in range(PASSES)]
        x_byte = held([P, T // 4], I32, "x_byte")
        w1_word = {e: held([P, PASSES, H // 2], I32, "w1_word%d" % e) for e in range(E) if e in (2, 3, 4, 6)}
        w1_head = held([P, 2, H // 2], I32, "w1_head")
        w1_late = [held([P, H // 2], I32, "w1_late%d" % e) for e in range(2)]
        w1_pass = {(e, o): held([P, H // 2], I32, "w1_pass%d_%d" % (e, o)) for e in BY_PASS for o in range(PASSES)}
        w1_byte = [held([P, 2 * PASSES, H // 4], I32, "w1_byte%d" % c) for c in range(PAIRS)]
        w2_word = [held([P, 2, N // 2], I32, "w2_word%d" % c) for c in range(PAIRS)]
        w2_byte = {run: held([P, run[1] - run[0], N // 4], I32, "w2_byte%d" % run[0]) for run in W2_BYTE_RUNS}
        slot_byte = {run: held([P, (run[1] - run[0]) * C], U8, "slot_byte%d" % run[0]) for run in BYTE_RUNS}
        moved_byte = {run: held([P, (run[1] - run[0]) * C // 4], I32, "moved_byte%d" % run[0]) for run in BYTE_RUNS}
        gate_col = held([P, GATE_COLS], F32, "gate_col")
        gate_sb = held([P, P, GATE_COLS], F32, "gate_sb")
        window = [held([P, T], F32, "window%d" % v) for v in range(2)]
        zero = held([P, 1], F32, "zero")
        ident = held([P, P], F32, "ident")
        acc_bank = [psum.tile([P, BANK], F32, name="acc_bank%d" % b) for b in range(4)]
        y_bank = [psum.tile([P, BANK], F32, name="y_bank%d" % b) for b in range(2)]
        turn_bank = [psum.tile([P, BANK], F32, name="turn_bank%d" % b) for b in range(2)]

        nc.gpsimd.memset(x_byte[:], 0)
        nc.vector.memset(ident[:], 0.0)
        nc.vector.memset(zero[:], 0.0)
        for plane in (w1_byte[0], moved_byte[0, 4], moved_byte[4, 8], w1_byte[1], w2_byte[0, 4], w1_byte[2], w1_byte[3], w2_byte[4, 8]):
            nc.vector.memset(plane[:], 0)
        make_identity(nc, ident[:], nomemset=True)

        def load_words(tile, words, a, b):
            nc.sync.dma_start(out=tile[:], in_=words[a:b].rearrange("e s p b -> p (e s) b").bitcast(I32))

        def load_scales(plane, scales, a, b):
            rows = scales[a:b].rearrange("e s (q r) i -> r q (e s) i", r=4)
            for r in range(4):
                nc.sync.dma_start(out=plane[r:P:32], in_=rows[r].bitcast(I32))

        def load_tokens(o):
            nc.sync.dma_start(out=x_word[o][:], in_=x_words[o].rearrange("p t r -> p (t r)").bitcast(I32))

        def load_w1(e):
            if e in BY_PASS:
                for o in range(PASSES):
                    nc.sync.dma_start(out=w1_pass[e, o][:], in_=w1_words[e, o].bitcast(I32))
            else:
                load_words(w1_word[e], w1_words, e, e + 1)

        def load_w1_scales(c):
            load_scales(w1_byte[c], w1_scales, 2 * c, 2 * c + 2)

        def load_w2(c):
            load_words(w2_word[c], w2_words, 2 * c, 2 * c + 2)

        def move_scales(run):
            nc.sync.dma_start(out=moved_byte[run][0 : P - SHIFT, :], in_=slot_byte[run][SHIFT:P, :].bitcast(I32))

        def slots_of(a, b):
            return offsets[:, a * C // 16 : b * C // 16]

        nc.sync.dma_start(offsets[:], offs)
        nc.sync.dma_start(out=w1_head[:], in_=w1_words[0:2, 0].rearrange("e p b -> p e b").bitcast(I32))
        token_rows = x_scales.rearrange("o (q r) t -> r q o t", r=4)
        for r in range(4):
            nc.sync.dma_start(out=x_byte[r:P:SHIFT, :], in_=token_rows[r].bitcast(I32))
        nc.sync.dma_start(out=gate_col[:], in_=gate[0].rearrange("(j c) -> j c", c=GATE_COLS))
        load_tokens(0)
        for run in BYTE_RUNS:
            nc.vector.tensor_copy(out=slot_byte[run][:], in_=x_byte[:].bitcast(U8).indirect(slots_of(*run)))
        load_w1_scales(0)
        load_tokens(1)
        move_scales(BYTE_RUNS[0])
        for e in range(2):
            nc.sync.dma_start(out=w1_late[e][:], in_=w1_words[e, 1].bitcast(I32))
        load_w1_scales(1)
        load_w1(2)
        load_w1(3)
        load_scales(w2_byte[0, 4], w2_scales, 0, 4)
        load_w2(0)
        load_w1(4)
        move_scales(BYTE_RUNS[1])
        load_w1_scales(2)
        load_w1(5)
        load_w2(1)
        load_w1(6)
        load_w1_scales(3)
        load_w1(7)
        load_scales(w2_byte[4, 8], w2_scales, 4, 8)
        load_w2(2)
        load_w2(3)

        slot_word = {}

        def gather_words(o, run, tag=None):
            slot_word[o, run] = held([P, (run[1] - run[0]) * C], U32, "slot_word%d_%d" % (o, run[0]), tag)
            nc.vector.tensor_copy(out=slot_word[o, run][:], in_=x_word[o][:].bitcast(U32).indirect(slots_of(*run)))

        for o in range(PASSES):
            for run in WORD_RUNS[o]:
                if o == 0 or run[0] < 5:
                    gather_words(o, run)

        for v in range(2):
            for a in range(0, T, CLEAR):
                nc.scalar.activation(out=window[v][:, a : a + CLEAR], in_=zero[:, 0:1].to_broadcast([P, CLEAR]), func=RELU)

        for b in range(2):
            for g in range(4):
                column = gate_col[:, 4 * b + g : 4 * b + g + 1].to_broadcast([P, P])
                nc.tensor.transpose(y_bank[b][:, g * P : (g + 1) * P], column, ident[:])
            nc.scalar.copy(out=gate_sb[:, :, 4 * b : 4 * b + 4], in_=y_bank[b][:].rearrange("p (g j) -> p j g", g=4))

        by_slot = {e: held([P, 2, P, 2], BF16, "by_slot%d" % e) for e in range(E) if e != 2}
        by_slot[2] = by_slot[1]
        h_bf = [held([P, 2 * C * 4], BF16, "h_bf%d" % c)[:].rearrange("p (m j t) -> p m j t", m=2, t=4) for c in range(PAIRS)]
        h_word = [held([P, 2 * C], U32, "h_word%d" % c) for c in range(PAIRS)]
        h_byte = [held([P, 2 * C], U8, "h_byte%d" % c) for c in range(PAIRS)]

        def as_words(e):
            return by_slot[e][:].rearrange("j u p d -> j (u p d)").bitcast(F32)

        def first_pass(e, o, acc, start, stop):
            words, rows = run_of(WORD_RUNS[o], e), run_of(BYTE_RUNS, e)
            plane = slot_byte[rows][:] if o == 0 else moved_byte[rows][:].bitcast(U8)
            if e < 2:
                weights = w1_late[e][:] if o else w1_head[:, e, :]
            else:
                weights = w1_pass[e, o][:] if e in BY_PASS else w1_word[e][:, o, :]
            nc.tensor.matmul_mx(
                out=acc[:],
                lhsT=slot_word[o, words][:, (e - words[0]) * C : (e - words[0] + 1) * C].bitcast(FP8X4),
                lhsT_scale=plane[:, (e - rows[0]) * C : (e - rows[0] + 1) * C],
                rhs=weights.bitcast(FP4X4),
                rhs_scale=w1_byte[e // 2][:, PASSES * (e % 2) + o, :].bitcast(U8),
                start=start,
                stop=stop,
            )

        def relu(e, words=slice(0, 2)):
            sums = acc_bank[ACC[e]][:].rearrange("j (p u d) -> j u p d", u=2, d=2)
            nc.scalar.activation(out=by_slot[e][:, words], in_=sums[:, words], func=RELU)

        def first_layer(e):
            for o in range(PASSES):
                first_pass(e, o, acc_bank[ACC[e]], o == 0, o == PASSES - 1)
            if e % 2 == 0:
                relu(e)
            else:
                for u in range(2):
                    relu(e, slice(u, u + 1))

        def regroup(e, turned):
            for u in range(2):
                nc.tensor.transpose(turned[:, u * C : (u + 1) * C], as_words(e)[:, u * P : (u + 1) * P], ident[:])
            nc.scalar.copy(out=h_bf[e // 2][:, e % 2].bitcast(F32), in_=turned.rearrange("p (u j) -> p j u", u=2))

        def quantise(c, a=0, b=2):
            values = h_bf[c][:, a:b].rearrange("p m j t -> p (m j t)")
            nc.vector.quantize_mx(out=h_word[c][:, a * C : b * C].bitcast(FP8X4), scales=h_byte[c][:, a * C : b * C], in_=values)

        def second_products(c, v, sums):
            for m in range(2):
                e = 2 * c + m
                rows = run_of(W2_BYTE_RUNS, e)
                nc.tensor.matmul_mx(
                    out=sums[:, m * C : (m + 1) * C],
                    lhsT=w2_word[c][:, m, v * P // 2 : (v + 1) * P // 2].bitcast(FP4X4),
                    lhsT_scale=w2_byte[rows][:, e - rows[0], v * P // 4 : (v + 1) * P // 4].bitcast(U8),
                    rhs=h_word[c][:, m * C : (m + 1) * C].bitcast(FP8X4),
                    rhs_scale=h_byte[c][:, m * C : (m + 1) * C],
                    start=True,
                    stop=True,
                )

        y_sb = {(0, 1): as_words(3), (1, 0): as_words(5)}
        for v in range(2):
            for c in range(PAIRS):
                if (c, v) not in y_sb:
                    y_sb[c, v] = held([P, 2 * C], F32, "y_sb%d_%d" % (c, v))[:]

        def gate_of(c):
            return gate_sb[:].rearrange("p j g -> p (j g)")[:, 2 * c * C : (2 * c + 2) * C]

        def scatter_times_gate(c, v):
            nc.vector.tensor_tensor(out=window[v][:].indirect(slots_of(2 * c, 2 * c + 2)), in0=y_sb[c, v], in1=gate_of(c), op=MULT)

        def lower_times_gate(c, sums):
            nc.vector.tensor_tensor(out=y_sb[c, 1], in0=sums, in1=gate_of(c), op=MULT)

        def scatter_lower(c):
            nc.scalar.activation(out=window[1][:].indirect(slots_of(2 * c, 2 * c + 2)), in_=y_sb[c, 1], func=COPY)

        def low(bank):
            return bank[:, 0 : BANK // 2]

        def high(bank):
            return bank[:, BANK // 2 : BANK]

        first_pass(0, 0, acc_bank[ACC[0]], True, False)
        first_pass(1, 0, acc_bank[ACC[1]], True, False)
        for repeat in range(WARM_UPS):
            first_pass(0, 0, acc_bank[3], True, True)
        first_pass(0, 1, acc_bank[ACC[0]], False, True)
        relu(0)
        first_pass(1, 1, acc_bank[ACC[1]], False, True)
        sums = acc_bank[ACC[1]][:].rearrange("j (p u d) -> j u p d", u=2, d=2)
        nc.vector.tensor_scalar_max(out=by_slot[1][:], in0=sums, scalar1=0.0)
        gather_words(1, (5, 7), "slot_word1_1")
        for e in range(2):
            regroup(e, low(turn_bank[e]))
            quantise(0, e, e + 1)
        gather_words(1, (7, 8), "h_bf0")

        first_layer(2)
        first_layer(3)
        second_products(0, 0, low(y_bank[0]))
        nc.vector.tensor_copy(out=y_sb[0, 0], in_=low(y_bank[0]))
        scatter_times_gate(0, 0)
        second_products(0, 1, high(turn_bank[0]))
        regroup(2, low(turn_bank[0]))
        regroup(3, high(y_bank[0]))
        quantise(1)
        nc.scalar.copy(out=y_sb[0, 1], in_=high(turn_bank[0]))
        scatter_times_gate(0, 1)

        first_layer(4)
        first_layer(5)
        second_products(1, 0, low(y_bank[1]))
        regroup(4, low(turn_bank[1]))
        regroup(5, low(turn_bank[0]))
        second_products(1, 1, high(y_bank[0]))
        quantise(2, 0, 1)
        lower_times_gate(1, high(y_bank[0]))
        quantise(2, 1, 2)
        nc.scalar.copy(out=y_sb[1, 0], in_=low(y_bank[1]))
        scatter_times_gate(1, 0)

        first_layer(6)
        first_layer(7)
        regroup(6, low(turn_bank[1]))
        quantise(3, 0, 1)
        second_products(2, 0, low(acc_bank[0]))
        second_products(2, 1, low(acc_bank[1]))
        lower_times_gate(2, low(acc_bank[1]))
        regroup(7, high(acc_bank[0]))
        nc.scalar.copy(out=y_sb[2, 0], in_=low(acc_bank[0]))
        quantise(3, 1, 2)
        scatter_times_gate(2, 0)
        scatter_lower(2)
        second_products(3, 0, low(y_bank[0]))
        nc.scalar.copy(out=y_sb[3, 0], in_=low(y_bank[0]))
        second_products(3, 1, low(acc_bank[2]))
        lower_times_gate(3, low(acc_bank[2]))
        scatter_times_gate(3, 0)
        nc.sync.dma_start(out=out[0:P, :], in_=window[0][:])
        scatter_lower(1)
        scatter_lower(3)
        nc.sync.dma_start(out=out[P : 2 * P, 0 : T // 2], in_=window[1][:, 0 : T // 2])
        nc.scalar.dma_start(out=out[P : 2 * P, T // 2 : T], in_=window[1][:, T // 2 : T])
